import numpy as np
import ml_dtypes


def mxq(x, axis, fmt="e4m3"):
    dtype, down = {"e4m3": (ml_dtypes.float8_e4m3fn, 7), "e5m2": (ml_dtypes.float8_e5m2, 14)}[fmt]
    v = np.moveaxis(np.asarray(x, np.float32).astype(ml_dtypes.bfloat16).astype(np.float64), axis, -1)
    blocks = v.reshape(v.shape[:-1] + (-1, 32))
    amax = np.abs(blocks).max(-1, keepdims=True)
    byte = np.maximum(np.where(amax > 0, np.frexp(amax)[1] - 1 + 127, 0) - down, 1)
    scale = np.exp2(byte - 127.0)
    codes = (blocks / scale).astype(np.float32).astype(dtype).astype(np.float64)
    return np.moveaxis((codes * scale).reshape(v.shape), -1, axis)


WIDE = False


def mx_kscale(k):
    if not WIDE:
        return np.ones(k)
    levels = np.array([10, -10, 5, -5, 0])
    if k % 512:
        return np.exp2(np.random.permutation(np.resize(levels, k // 32))).repeat(32)
    a = np.empty((k // 512, 16))
    for p in range(k // 512):
        a[p, :8] = np.random.permutation(np.resize(levels, 8))
        for g in range(8):
            far = levels[np.abs(levels - a[p, g]) >= 10]
            a[p, g + 8] = far[np.random.randint(len(far))]
    return np.exp2(a.ravel()).repeat(32)


BF16 = ml_dtypes.bfloat16


def bf(x):
    return np.asarray(x, np.float32).astype(BF16)


def f64(x):
    return np.asarray(x).astype(np.float64)


E2M1 = np.array([0.0, 0.5, 1.0, 1.5, 2.0, 3.0, 4.0, 6.0, -0.0, -0.5, -1.0, -1.5, -2.0, -3.0, -4.0, -6.0])


def pack_weight(w, fmt):
    k, n = w.shape
    w = f64(bf(w)).reshape(k // 32, 32, n)
    amax = np.abs(w).max(1)
    if fmt == "e4m3":
        byte = np.frexp(amax)[1] - 1 + 127 - 7
    else:
        mant, ex = np.frexp(amax / 6.0)
        byte = np.where(mant > 0.5, ex, ex - 1) + 127
    byte = np.clip(np.where(amax > 0, byte, 1), 1, 254)
    scaled = (w * np.exp2(127.0 - byte)[:, None, :]).reshape(k, n).astype(np.float32)
    by_word = np.ascontiguousarray(scaled.reshape(k // 512, 128, 4, n).transpose(0, 1, 3, 2))
    if fmt == "e4m3":
        words = by_word.astype(ml_dtypes.float8_e4m3fn).view(np.uint8)
    else:
        c = by_word.astype(ml_dtypes.float4_e2m1fn).view(np.uint8) & 0xF
        words = c[..., 0::2] | (c[..., 1::2] << 4)
    return np.ascontiguousarray(words), np.ascontiguousarray(byte.astype(np.uint8).reshape(k // 512, 16, n))


def unpack_weight(words, scales, fmt):
    g, p, n, _ = words.shape
    if fmt == "e4m3":
        vals = np.ascontiguousarray(words).view(ml_dtypes.float8_e4m3fn).astype(np.float64)
    else:
        nib = np.empty((g, p, n, 4), np.uint8)
        nib[..., 0::2] = words & 0xF
        nib[..., 1::2] = words >> 4
        vals = E2M1[nib]
    vals = vals * np.repeat(np.exp2(scales.astype(np.float64) - 127.0), 8, axis=1)[..., None]
    return vals.transpose(0, 1, 3, 2).reshape(g * 512, n)
def pack4(w):
    words, scales = pack_weight(w, "e2m1")
    return words.reshape(words.shape[0], 128, -1), scales


def unpack4(words, scales):
    return unpack_weight(words.reshape(words.shape[0], 128, -1, 2), scales, "e2m1")


E4M3FN = np.array([(-1.0 if i & 128 else 1.0) * ((1.0 + (i & 7) / 8.0) * 2.0 ** (((i >> 3) & 15) - 7) if i & 120 else (i & 7) * 2.0 ** -9) for i in range(256)])


def e4m3fn_bytes(y):
    return np.clip(np.asarray(y, np.float64), -448.0, 448.0).astype(np.float32).astype(ml_dtypes.float8_e4m3fn).view(np.uint8)


def e4m3fn_values(b):
    return E4M3FN[b]

def planes(Y):
    n, m = Y.shape
    b = f64(bf(Y)).reshape(n // 32, 32, m)
    amax = np.abs(b).max(1)
    byte = np.clip(np.where(amax > 0, np.frexp(amax)[1] - 1 + 127 - 7, 1), 1, 254)
    codes = (b * np.exp2(127.0 - byte)[:, None, :]).reshape(n, m).astype(np.float32).astype(ml_dtypes.float8_e4m3fn).view(np.uint8)
    words = codes.reshape(n // 512, 128, 4, m).transpose(0, 1, 3, 2)
    return np.ascontiguousarray(words), np.ascontiguousarray(byte.astype(np.uint8).reshape(n // 512, 16, m))


T, S, D, DV = 1024, 2048, 1024, 1024
E4M3_MAX = 448.0

def setup_inputs():
    s = mx_kscale(D)
    t = mx_kscale(S)
    qt = np.random.randn(D, T) * (1.2 / np.sqrt(D)) * s[:, None]
    qry_words, qry_scales = pack_weight(qt, "e4m3")
    keys = np.random.randn(S, D) * np.exp(0.5 * np.random.randn(1, D)) / s[None, :]
    keys_scale = (np.abs(keys).max(axis=0, keepdims=True) / E4M3_MAX).astype(np.float32)
    keys_bytes = e4m3fn_bytes(keys / np.repeat(f64(keys_scale), S, axis=0))
    key_bias = bf(-1.0 + 0.3 * np.random.randn(1, S))
    key_gain = bf((1.0 + 0.1 * np.random.randn(1, S)) * t[None, :])
    vals = np.random.randn(S, DV) * (3.0 / np.sqrt(S)) * np.exp(0.8 * np.random.randn(1, DV))
    vals = bf(vals / t[:, None])
    gate = bf(1.0 + 0.3 * np.random.randn(T, DV))
    return {"qry_words": qry_words, "qry_scales": qry_scales,
            "keys_bytes": keys_bytes, "keys_scale": keys_scale,
            "key_bias": key_bias, "key_gain": key_gain,
            "vals": vals, "gate": gate}

def reference(qry_words, qry_scales, keys_bytes, keys_scale, key_bias, key_gain, vals, gate):
    qt = unpack_weight(qry_words, qry_scales, "e4m3")
    keys = e4m3fn_values(keys_bytes) * np.repeat(f64(keys_scale), S, axis=0)
    logits = qt.T @ mxq(keys, 1, "e4m3").T
    a = f64(key_gain) / (1.0 + np.exp(-(logits + f64(key_bias))))
    o = mxq(a, 1, "e4m3") @ mxq(f64(vals), 0, "e4m3")
    y = o * f64(gate)
    words, scales = planes(y.T)
    return y, words, scales

@@ -1,0 +1,443 @@
+from contextlib import ExitStack
+
+import concourse.mybir as mybir
+from concourse.masks import make_identity
+
+T, S, D, DV = 1024, 2048, 1024, 1024
+FLOPS = 2 * T * S * D + 2 * T * S * DV
+
+F32 = mybir.dt.float32
+BF16 = mybir.dt.bfloat16
+U32 = mybir.dt.uint32
+I32 = mybir.dt.int32
+U8 = mybir.dt.uint8
+FP8 = mybir.dt.float8_e4m3fn
+FP8X4 = mybir.dt.float8_e4m3fn_x4
+MULT = mybir.AluOpType.mult
+SIGMOID = mybir.ActivationFunctionType.Sigmoid
+
+P = 128
+W = 512
+
+
+def tile_gated_sigmoid_attention_b7_kernel(
+    tc, qry_words, qry_scales, keys_bytes, keys_scale, key_bias, key_gain, vals, gate, out_0, out_1, out_2
+):
+    nc = tc.nc
+    with ExitStack() as ctx:
+        keep = ctx.enter_context(tc.tile_pool(name="keep", bufs=1))
+        work = ctx.enter_context(tc.tile_pool(name="work", bufs=2))
+        psum = ctx.enter_context(tc.psum_pool(name="psum", bufs=1))
+        ctx.enter_context(tc.manual_schedule())
+
+        def bank(i):
+            return psum.tile([P, W], F32, name="bank%d" % i)
+
+        def kept(name, width, dtype):
+            return keep.tile([P, width], dtype, name=name, align_bytes=64)
+
+        def passing(name, width, dtype, bufs):
+            return work.tile([P, width], dtype, name=name, bufs=bufs, align_bytes=64)
+
+        def quantize(name, grouped):
+            width = grouped.shape[1] // 4
+            codes = kept(name + "_codes", width, U32)
+            scales = kept(name + "_scales", width, U8)
+            nc.vector.quantize_mx(out=codes[:].bitcast(FP8X4), scales=scales[:], in_=grouped[:])
+            return codes, scales
+
+        key_rows = keys_bytes.rearrange("(G m a j) k -> G a m (j k)", m=P, a=2, j=2)
+        key_tiles, val_raw, gate_tiles, q_codes = {}, {}, {}, {}
+
+        def load_keys(n):
+            key_tiles[n] = kept("key_bytes%d" % n, 2 * D, U8)
+            nc.sync.dma_start(out=key_tiles[n][:], in_=key_rows[n // 2, n % 2])
+
+        def load_vals(G, h):
+            val_raw[G, h] = work.tile([P, 4 * W], BF16, name="val_raw%d" % G, bufs=1)
+            nc.sync.dma_start(
+                out=val_raw[G, h][:].rearrange("p (t w) -> p t w", t=4),
+                in_=vals[G * W : (G + 1) * W, h * W : (h + 1) * W].rearrange("(p t) w -> p t w", t=4),
+            )
+
+        def load_gate(b, h):
+            gate_tiles[b, h] = work.tile([P, 4 * W], BF16, name="gate%d" % ((2 * b + h) % 3), bufs=1)
+            nc.sync.dma_start(
+                out=gate_tiles[b, h][:].rearrange("p (j w) -> p j w", j=4),
+                in_=gate[b * W : (b + 1) * W, h * W : (h + 1) * W].rearrange("(j p) w -> p j w", p=P),
+            )
+
+        def load_queries(b):
+            q_codes[b] = kept("q_codes%d" % b, 2 * W, U32)
+            nc.sync.dma_start(
+                out=q_codes[b][:].bitcast(I32).rearrange("p (g n) -> p g n", g=2),
+                in_=qry_words.rearrange("g p n t -> p g (n t)")[:, :, b * 4 * W : (b + 1) * 4 * W].bitcast(I32),
+            )
+
+        scale_cols = kept("scale_cols", 8, F32)
+        nc.sync.dma_start(out=scale_cols[:], in_=keys_scale.rearrange("o (p c) -> p (o c)", c=8))
+        ident = kept("ident", P, F32)
+        make_identity(nc, ident[:])
+        q_scales = kept("q_scales", 2 * T, U8)
+        nc.gpsimd.memset(q_scales[:].bitcast(I32), 0)
+        warm = kept("warm", 1, F32)
+        nc.scalar.activation(out=warm[:], in_=ident[:, 0:1], func=SIGMOID)
+
+        load_keys(0)
+        load_vals(0, 0)
+        load_keys(1)
+        load_keys(2)
+        load_vals(1, 0)
+        load_keys(3)
+        load_queries(0)
+        for Q in range(4):
+            nc.sync.dma_start(
+                out=q_scales[32 * Q : 32 * Q + 4, :].bitcast(I32).rearrange("r (g n) -> r g n", g=2),
+                in_=qry_scales[:, 4 * Q : 4 * Q + 4, :].rearrange("g r n -> r g n").bitcast(I32),
+            )
+        bias = kept("bias", 16, BF16)
+        gain = kept("gain", 16, BF16)
+        nc.sync.dma_start(
+            out=bias[:].rearrange("m (G t) -> m G t", t=4), in_=key_bias.rearrange("o (G m t) -> m (o G) t", m=P, t=4)
+        )
+        nc.sync.dma_start(
+            out=gain[:].rearrange("m (G t) -> m G t", t=4), in_=key_gain.rearrange("o (G m t) -> m (o G) t", m=P, t=4)
+        )
+        load_keys(4)
+        load_vals(2, 0)
+        load_keys(5)
+        load_keys(6)
+        load_vals(3, 0)
+        load_keys(7)
+        load_queries(1)
+        load_gate(0, 0)
+
+        scale_all = kept("scale_all", D, F32)
+        for half in range(2):
+            spread = bank(half)
+            for c in range(4):
+                col = 4 * half + c
+                nc.tensor.transpose(
+                    spread[:, c * P : (c + 1) * P], scale_cols[:, col : col + 1].to_broadcast([P, P]), ident[:]
+                )
+            dst = scale_all[:].rearrange("q (p c) -> q p c", c=8)[:, :, 4 * half : 4 * half + 4]
+            src = spread[:].rearrange("q (c p) -> q p c", c=4)
+            if half == 0:
+                nc.scalar.copy(out=dst, in_=src)
+            else:
+                nc.vector.tensor_copy(out=dst, in_=src)
+
+        tiles = {}
+        y_scales = kept("y_scales", 2 * T, U8)
+        free = {
+            "key_wide": [0, 1, 2, 3],
+            "key_grouped": [0, 1, 2],
+            "val_grouped": [0, 1, 2, 3],
+            "sig": [0, 1, 2, 3, 4, 5],
+            "att_grouped": [0, 1],
+            "y": [0, 1, 2, 3, 4, 5],
+            "y_rounded": [0, 1, 2, 3],
+            "y_grouped": [0, 1],
+            "logit_bank": [0, 1, 2],
+            "key_bank": [3, 4, 5, 6],
+            "sum_bank": [],
+            "y_bank": [7],
+        }
+        slot_of = {}
+
+        def take(kind, key, width=W, dtype=F32):
+            slot = free[kind][0]
+            free[kind].remove(slot)
+            slot_of[kind, key] = slot
+            if "bank" in kind:
+                tiles[kind, key] = bank(slot)
+            else:
+                tiles[kind, key] = work.tile([P, width], dtype, name="%s%d" % (kind, slot), bufs=1, align_bytes=64)
+            return tiles[kind, key]
+
+        def give(kind, key, to=None):
+            free[to or kind].append(slot_of[kind, key])
+
+        key_q, val_q, att_q = {}, {}, {}
+
+        def widen_keys(i):
+            wide = take("key_wide", i, D, BF16)
+            nc.vector.tensor_tensor(
+                out=wide[:], in0=key_tiles[i // 2][:, (i % 2) * D : (i % 2 + 1) * D].bitcast(FP8), in1=scale_all[:], op=MULT
+            )
+
+        def turn_keys(i):
+            words = tiles["key_wide", i][:].bitcast(F32)
+            turned = take("key_bank", i)
+            for g in range(2):
+                for u in range(2):
+                    c = 2 * g + u
+                    nc.tensor.transpose(
+                        turned[:, c * P : (c + 1) * P], words[:, 256 * g + u : 256 * (g + 1) : 2], ident[:]
+                    )
+            give("key_wide", i)
+
+        def group_keys(i):
+            n, j = divmod(i, 2)
+            if j == 0:
+                take("key_grouped", n, 2 * D, BF16)
+            nc.scalar.copy(
+                out=tiles["key_grouped", n][:].bitcast(F32)[:, j * W : (j + 1) * W].rearrange("p (g m u) -> p g m u", g=2, u=2),
+                in_=tiles["key_bank", i][:].rearrange("p (g u m) -> p g m u", g=2, u=2),
+            )
+            give("key_bank", i, "sum_bank" if i >= 12 else None)
+
+        def quantize_keys(n):
+            key_q[n] = quantize("key%d" % n, tiles["key_grouped", n])
+            give("key_grouped", n)
+
+        def group_vals(G, h):
+            grouped = take("val_grouped", (G, h), 4 * W, BF16)
+            nc.scalar.copy(
+                out=grouped[:].rearrange("p (c i t) -> p c t i", i=4, t=4),
+                in_=val_raw[G, h][:].rearrange("p (t c i) -> p c t i", i=4, t=4),
+            )
+            if h == 0:
+                load_vals(G, 1)
+            if (G, h) == (3, 0):
+                load_gate(0, 1)
+                load_gate(1, 0)
+
+        def quantize_vals(G, h):
+            val_q[G, h] = quantize("val%d_%d" % (G, h), tiles["val_grouped", (G, h)])
+            give("val_grouped", (G, h))
+
+        def logits(G, b, t):
+            codes, scales = key_q[2 * G + t // 2]
+            out = take("logit_bank", (G, b, t))
+            for g in range(2):
+                cols = slice((t % 2) * 256 + g * P, (t % 2) * 256 + (g + 1) * P)
+                nc.tensor.matmul_mx(
+                    out=out[:],
+                    lhsT=codes[:, cols].bitcast(FP8X4),
+                    lhsT_scale=scales[:, cols],
+                    rhs=q_codes[b][:, g * W : (g + 1) * W].bitcast(FP8X4),
+                    rhs_scale=q_scales[:, g * T + b * W : g * T + (b + 1) * W],
+                    start=(g == 0),
+                    stop=(g == 1),
+                )
+
+        def sigmoid(G, b, t):
+            if t == 0:
+                take("sig", (G, b), 4 * W, F32)
+            nc.scalar.activation(
+                out=tiles["sig", (G, b)][:, t * W : (t + 1) * W],
+                in_=tiles["logit_bank", (G, b, t)][:],
+                func=SIGMOID,
+                bias=bias[:, 4 * G + t : 4 * G + t + 1],
+            )
+            last = (G, b) == (3, 1) and t >= 1
+            give("logit_bank", (G, b, t), ("y_bank" if t == 1 else "sum_bank") if last else None)
+
+        def apply_gain(G, b):
+            grouped = take("att_grouped", (G, b), 4 * W, BF16)
+            nc.vector.tensor_tensor(
+                out=grouped[:].rearrange("p (c i t) -> p c t i", i=4, t=4),
+                in0=tiles["sig", (G, b)][:].rearrange("p (t c i) -> p c t i", i=4, t=4),
+                in1=gain[:, 4 * G : 4 * G + 4].unsqueeze(1).unsqueeze(3).to_broadcast([P, W // 4, 4, 4]),
+                op=MULT,
+            )
+            give("sig", (G, b))
+
+        def quantize_att(G, b):
+            att_q[G, b] = quantize("att%d_%d" % (G, b), tiles["att_grouped", (G, b)])
+            give("att_grouped", (G, b))
+
+        def mix(j, h, G):
+            if G == 0:
+                take("sum_bank", (j, h))
+            codes, scales = att_q[G, j // 4]
+            cols = slice((j % 4) * P, (j % 4 + 1) * P)
+            nc.tensor.matmul_mx(
+                out=tiles["sum_bank", (j, h)][:],
+                lhsT=codes[:, cols].bitcast(FP8X4),
+                lhsT_scale=scales[:, cols],
+                rhs=val_q[G, h][0][:].bitcast(FP8X4),
+                rhs_scale=val_q[G, h][1][:],
+                start=(G == 0),
+                stop=(G == 3),
+            )
+
+        def apply_gate(j, h):
+            y = take("y", (j, h))
+            nc.vector.tensor_tensor(
+                out=y[:],
+                in0=tiles["sum_bank", (j, h)][:],
+                in1=gate_tiles[j // 4, h][:, (j % 4) * W : (j % 4 + 1) * W],
+                op=MULT,
+            )
+            give("sum_bank", (j, h))
+            nc.sync.dma_start(out=out_0[j * P : (j + 1) * P, h * W : (h + 1) * W], in_=y[:])
+            if (j, h) == (3, 0):
+                load_gate(1, 1)
+
+        def round_y(j, h, engine):
+            rounded = take("y_rounded", (j, h), W, BF16)
+            dst = rounded[:].rearrange("p (u m e) -> p u m e", u=2, e=2)
+            src = tiles["y", (j, h)][:].rearrange("p (m u e) -> p u m e", u=2, e=2)
+            if engine == "V":
+                nc.vector.tensor_copy(out=dst, in_=src)
+            else:
+                nc.scalar.copy(out=dst, in_=src)
+            give("y", (j, h))
+
+        def turn_y(j, h):
+            if j % 2 == 0:
+                take("y_bank", (j // 2, h))
+            words = tiles["y_rounded", (j, h)][:].bitcast(F32)
+            for u in range(2):
+                c = 2 * (j % 2) + u
+                nc.tensor.transpose(
+                    tiles["y_bank", (j // 2, h)][:, c * P : (c + 1) * P], words[:, u * P : (u + 1) * P], ident[:]
+                )
+            give("y_rounded", (j, h))
+
+        def group_y(pair, h):
+            grouped = take("y_grouped", (pair, h), 2 * W, BF16)
+            nc.scalar.copy(
+                out=grouped[:].bitcast(F32).rearrange("p (j r u) -> p j r u", j=2, u=2),
+                in_=tiles["y_bank", (pair, h)][:].rearrange("p (j u r) -> p j r u", j=2, u=2),
+            )
+            give("y_bank", (pair, h))
+
+        def quantize_y(pair, h):
+            codes = passing("y_codes", 2 * P, U32, 3)
+            cols = slice(h * T + pair * 2 * P, h * T + (pair + 1) * 2 * P)
+            nc.vector.quantize_mx(
+                out=codes[:].bitcast(FP8X4), scales=y_scales[:, cols], in_=tiles["y_grouped", (pair, h)][:]
+            )
+            give("y_grouped", (pair, h))
+            nc.sync.dma_start(
+                out=out_1[h].rearrange("p m t -> p (m t)")[:, pair * 8 * P : (pair + 1) * 8 * P].bitcast(I32),
+                in_=codes[:].bitcast(I32),
+            )
+
+        def needs(step):
+            fn, a = step[0], step[1:]
+            if fn is widen_keys:
+                return [], "key_wide"
+            if fn is turn_keys:
+                return [(widen_keys, *a)], "key_bank"
+            if fn is group_keys:
+                return [(turn_keys, *a)], ("key_grouped" if a[0] % 2 == 0 else None)
+            if fn is quantize_keys:
+                return [(group_keys, 2 * a[0] + 1)], None
+            if fn is group_vals:
+                return [], "val_grouped"
+            if fn is quantize_vals:
+                return [(group_vals, *a)], None
+            if fn is logits:
+                return [(quantize_keys, 2 * a[0] + a[2] // 2)], "logit_bank"
+            if fn is sigmoid:
+                return [(logits, *a)], ("sig" if a[2] == 0 else None)
+            if fn is apply_gain:
+                return [(sigmoid, *a, 3)], "att_grouped"
+            if fn is quantize_att:
+                return [(apply_gain, *a)], None
+            if fn is mix:
+                return [(quantize_att, a[2], a[0] // 4), (quantize_vals, a[2], a[1])], ("sum_bank" if a[2] == 0 else None)
+            if fn is apply_gate:
+                return [(mix, *a, 3)], "y"
+            if fn is round_y:
+                return [(apply_gate, a[0], a[1])], "y_rounded"
+            if fn is turn_y:
+                return [(round_y, *a, round_engine(*a))], ("y_bank" if a[0] % 2 == 0 else None)
+            if fn is group_y:
+                return [(turn_y, 2 * a[0] + 1, a[1])], "y_grouped"
+            return [(group_y, *a)], None
+
+        def round_engine(j, h):
+            return "V" if (h == 1 and j >= 6) else "S"
+
+        def sig_unit(G, b):
+            return [(sigmoid, G, b, t) for t in range(4)]
+
+        def logit_unit(G, b):
+            return [(logits, G, b, t) for t in range(4)]
+
+        def rounds(pair, h):
+            return [(round_y, j, h, "S") for j in (2 * pair, 2 * pair + 1) if round_engine(j, h) == "S"]
+
+        A = [(j, 0) for j in range(4)]
+        B = [(j, 1) for j in range(4)]
+        C = [(j, 0) for j in range(4, 8)]
+        E = [(j, 1) for j in range(4, 8)]
+
+        def gates(units):
+            return [(apply_gate, j, h) for j, h in units]
+
+        def mixes(units, Gs):
+            return [(mix, j, h, G) for G in Gs for j, h in units]
+
+        def turns(units):
+            return [(turn_y, j, h) for j, h in units]
+
+        vector = []
+        for n in range(8):
+            vector += [(widen_keys, 2 * n), (widen_keys, 2 * n + 1)]
+            if n >= 2:
+                vector += [(quantize_keys, n - 2)]
+        vector += [(quantize_keys, 6), (apply_gain, 0, 0), (quantize_keys, 7), (quantize_vals, 0, 0), (quantize_att, 0, 0)]
+        for G in range(1, 4):
+            vector += [(apply_gain, G, 0), (quantize_vals, G, 0), (quantize_att, G, 0)]
+        vector += [(apply_gain, 0, 1)] + gates(A[:2]) + [(quantize_att, 0, 1)] + gates(A[2:])
+        vector += [(quantize_vals, 0, 1), (quantize_vals, 1, 1), (apply_gain, 1, 1), (quantize_vals, 2, 1), (quantize_att, 1, 1), (quantize_vals, 3, 1)]
+        vector += [(apply_gain, 2, 1)] + gates(B[:2]) + [(quantize_att, 2, 1)] + gates(B[2:]) + [(quantize_y, 0, 0)]
+        vector += [(apply_gain, 3, 1), (quantize_y, 1, 0), (quantize_att, 3, 1), (quantize_y, 0, 1)]
+        vector += gates(C[:2]) + [(quantize_y, 1, 1)] + gates(C[2:]) + gates(E[:2]) + [(quantize_y, 2, 0)]
+        vector += gates(E[2:]) + [(round_y, 6, 1, "V"), (round_y, 7, 1, "V")]
+        vector += [(quantize_y, 3, 0), (quantize_y, 2, 1), (quantize_y, 3, 1)]
+
+        extras = [[(group_vals, 1, 0)], [(group_vals, 2, 0)], [], sig_unit(0, 0), sig_unit(0, 1), [], sig_unit(1, 0), sig_unit(1, 1)]
+        scalar = [(group_vals, 0, 0)]
+        for n in range(8):
+            scalar += [(group_keys, 2 * n), (group_keys, 2 * n + 1)] + extras[n]
+        scalar += sig_unit(2, 0) + sig_unit(3, 0) + [(group_vals, 3, 0)] + sig_unit(2, 1) + [(group_vals, 0, 1), (group_vals, 1, 1)] + sig_unit(3, 1)
+        scalar += [(group_vals, G, 1) for G in range(2, 4)]
+        pairs = [(0, 0), (1, 0), (0, 1), (1, 1), (2, 0), (3, 0), (2, 1), (3, 1)]
+        for i in range(9):
+            if i == 4:
+                scalar += [(group_y, *pairs[i - 1])]
+            if i < 8:
+                scalar += rounds(*pairs[i])
+            if i > 0 and i != 4:
+                scalar += [(group_y, *pairs[i - 1])]
+
+        tensor = []
+        for n in range(8):
+            tensor += [(turn_keys, 2 * n), (turn_keys, 2 * n + 1)] + [(logits, *s[1:]) for s in extras[n] if s[0] is sigmoid]
+        tensor += logit_unit(2, 0) + logit_unit(3, 0) + logit_unit(2, 1)[:2] + mixes(A, [0, 1]) + logit_unit(2, 1)[2:]
+        tensor += mixes(A, [2]) + logit_unit(3, 1)[:3] + mixes(A, [3]) + logit_unit(3, 1)[3:]
+        tensor += mixes(B, [0, 1]) + mixes(C[:2], [0]) + mixes(B, [2, 3]) + mixes(C[:2], [1]) + turns(A)
+        tensor += mixes(C[2:], [0, 1]) + mixes(C, [2]) + mixes(E[:2], [0, 1, 2]) + turns(B)
+        tensor += mixes(C, [3]) + mixes(E[:2], [3])
+        tensor += mixes(E[2:3], range(4)) + turns(C[:2]) + mixes(E[3:], range(4)) + turns(C[2:]) + turns(E)
+
+
+        queues = [vector, scalar, tensor]
+        done = set()
+        while any(queues):
+            moved = False
+            for queue in queues:
+                while queue:
+                    before, kind = needs(queue[0])
+                    if not (all(x in done for x in before) and (kind is None or free[kind])):
+                        break
+                    step = queue[0]
+                    queue.remove(step)
+                    step[0](*step[1:])
+                    done.add(step)
+                    moved = True
+            assert moved, [(q[0][0], q[0][1:]) for q in queues if q]
+
+        for Q in range(4):
+            dma_queue = nc.sync if Q % 2 == 0 else nc.scalar
+            dma_queue.dma_start(
+                out=out_2[:, 4 * Q : 4 * Q + 4, :].rearrange("g r m -> r g m").bitcast(I32),
+                in_=y_scales[32 * Q : 32 * Q + 4, :].bitcast(I32).rearrange("r (g m) -> r g m", g=2),
+            )

@@ -50,7 +50,7 @@ def tile_gated_sigmoid_attention_b7_kernel(
         key_tiles, val_raw, gate_tiles, q_codes = {}, {}, {}, {}
 
         def load_keys(n):
-            key_tiles[n] = kept("key_bytes%d" % n, 2 * D, U8)
+            key_tiles[n] = work.tile([P, 2 * D], U8, name="key_bytes%d" % (n % 6), bufs=1)
             nc.sync.dma_start(out=key_tiles[n][:], in_=key_rows[n // 2, n % 2])
 
         def load_vals(G, h):
@@ -83,12 +83,14 @@ def tile_gated_sigmoid_attention_b7_kernel(
         warm = kept("warm", 1, F32)
         nc.scalar.activation(out=warm[:], in_=ident[:, 0:1], func=SIGMOID)
 
-        load_keys(0)
         load_vals(0, 0)
+        load_keys(0)
+        load_vals(1, 0)
         load_keys(1)
         load_keys(2)
-        load_vals(1, 0)
+        load_vals(2, 0)
         load_keys(3)
+        load_vals(3, 0)
         load_queries(0)
         for Q in range(4):
             nc.sync.dma_start(
@@ -104,13 +106,8 @@ def tile_gated_sigmoid_attention_b7_kernel(
             out=gain[:].rearrange("m (G t) -> m G t", t=4), in_=key_gain.rearrange("o (G m t) -> m (o G) t", m=P, t=4)
         )
         load_keys(4)
-        load_vals(2, 0)
         load_keys(5)
-        load_keys(6)
-        load_vals(3, 0)
-        load_keys(7)
         load_queries(1)
-        load_gate(0, 0)
 
         scale_all = kept("scale_all", D, F32)
         for half in range(2):
@@ -122,10 +119,7 @@ def tile_gated_sigmoid_attention_b7_kernel(
                 )
             dst = scale_all[:].rearrange("q (p c) -> q p c", c=8)[:, :, 4 * half : 4 * half + 4]
             src = spread[:].rearrange("q (c p) -> q p c", c=4)
-            if half == 0:
-                nc.scalar.copy(out=dst, in_=src)
-            else:
-                nc.vector.tensor_copy(out=dst, in_=src)
+            nc.scalar.copy(out=dst, in_=src)
 
         tiles = {}
         y_scales = kept("y_scales", 2 * T, U8)
@@ -137,7 +131,7 @@ def tile_gated_sigmoid_attention_b7_kernel(
             "att_grouped": [0, 1],
             "y": [0, 1, 2, 3, 4, 5],
             "y_rounded": [0, 1, 2, 3],
-            "y_grouped": [0, 1],
+            "y_grouped": [0, 1, 2],
             "logit_bank": [0, 1, 2],
             "key_bank": [3, 4, 5, 6],
             "sum_bank": [],
@@ -165,6 +159,8 @@ def tile_gated_sigmoid_attention_b7_kernel(
             nc.vector.tensor_tensor(
                 out=wide[:], in0=key_tiles[i // 2][:, (i % 2) * D : (i % 2 + 1) * D].bitcast(FP8), in1=scale_all[:], op=MULT
             )
+            if i in (1, 3):
+                load_keys(6 + i // 2)
 
         def turn_keys(i):
             words = tiles["key_wide", i][:].bitcast(F32)
@@ -193,13 +189,16 @@ def tile_gated_sigmoid_attention_b7_kernel(
 
         def group_vals(G, h):
             grouped = take("val_grouped", (G, h), 4 * W, BF16)
-            nc.scalar.copy(
-                out=grouped[:].rearrange("p (c i t) -> p c t i", i=4, t=4),
-                in_=val_raw[G, h][:].rearrange("p (t c i) -> p c t i", i=4, t=4),
-            )
+            dst = grouped[:].rearrange("p (c i t) -> p c t i", i=4, t=4)
+            src = val_raw[G, h][:].rearrange("p (t c i) -> p c t i", i=4, t=4)
+            if (G, h) == (0, 0):
+                nc.vector.tensor_copy(out=dst, in_=src)
+            else:
+                nc.scalar.copy(out=dst, in_=src)
             if h == 0:
                 load_vals(G, 1)
             if (G, h) == (3, 0):
+                load_gate(0, 0)
                 load_gate(0, 1)
                 load_gate(1, 0)
 
@@ -306,7 +305,7 @@ def tile_gated_sigmoid_attention_b7_kernel(
             give("y_bank", (pair, h))
 
         def quantize_y(pair, h):
-            codes = passing("y_codes", 2 * P, U32, 3)
+            codes = passing("y_codes", 2 * P, U32, 4)
             cols = slice(h * T + pair * 2 * P, h * T + (pair + 1) * 2 * P)
             nc.vector.quantize_mx(
                 out=codes[:].bitcast(FP8X4), scales=y_scales[:, cols], in_=tiles["y_grouped", (pair, h)][:]
@@ -378,48 +377,44 @@ def tile_gated_sigmoid_attention_b7_kernel(
             return [(turn_y, j, h) for j, h in units]
 
         vector = []
+        vector += [(group_vals, 0, 0)]
         for n in range(8):
             vector += [(widen_keys, 2 * n), (widen_keys, 2 * n + 1)]
             if n >= 2:
                 vector += [(quantize_keys, n - 2)]
-        vector += [(quantize_keys, 6), (apply_gain, 0, 0), (quantize_keys, 7), (quantize_vals, 0, 0), (quantize_att, 0, 0)]
+        vector += [(quantize_keys, 6), (apply_gain, 0, 0), (quantize_vals, 0, 0), (quantize_keys, 7), (quantize_att, 0, 0)]
         for G in range(1, 4):
             vector += [(apply_gain, G, 0), (quantize_vals, G, 0), (quantize_att, G, 0)]
-        vector += [(apply_gain, 0, 1)] + gates(A[:2]) + [(quantize_att, 0, 1)] + gates(A[2:])
-        vector += [(quantize_vals, 0, 1), (quantize_vals, 1, 1), (apply_gain, 1, 1), (quantize_vals, 2, 1), (quantize_att, 1, 1), (quantize_vals, 3, 1)]
-        vector += [(apply_gain, 2, 1)] + gates(B[:2]) + [(quantize_att, 2, 1)] + gates(B[2:]) + [(quantize_y, 0, 0)]
-        vector += [(apply_gain, 3, 1), (quantize_y, 1, 0), (quantize_att, 3, 1), (quantize_y, 0, 1)]
-        vector += gates(C[:2]) + [(quantize_y, 1, 1)] + gates(C[2:]) + gates(E[:2]) + [(quantize_y, 2, 0)]
-        vector += gates(E[2:]) + [(round_y, 6, 1, "V"), (round_y, 7, 1, "V")]
-        vector += [(quantize_y, 3, 0), (quantize_y, 2, 1), (quantize_y, 3, 1)]
+        vector += [(quantize_vals, 0, 1), (quantize_vals, 1, 1)] + gates(A)
+        vector += [(apply_gain, 0, 1), (quantize_vals, 2, 1), (quantize_vals, 3, 1), (quantize_att, 0, 1)]
+        vector += [(apply_gain, 1, 1)] + gates(B[:2]) + [(quantize_att, 1, 1)] + gates(B[2:])
+        vector += [(apply_gain, 2, 1), (quantize_y, 0, 0), (quantize_att, 2, 1), (quantize_y, 1, 0)]
+        vector += [(apply_gain, 3, 1), (quantize_y, 0, 1), (quantize_att, 3, 1), (quantize_y, 1, 1)]
+        vector += gates(C) + gates(E) + [(round_y, 6, 1, "V"), (round_y, 7, 1, "V")]
+        vector += [(quantize_y, 2, 0), (quantize_y, 3, 0), (quantize_y, 2, 1), (quantize_y, 3, 1)]
 
-        extras = [[(group_vals, 1, 0)], [(group_vals, 2, 0)], [], sig_unit(0, 0), sig_unit(0, 1), [], sig_unit(1, 0), sig_unit(1, 1)]
-        scalar = [(group_vals, 0, 0)]
+        extras = [[(group_vals, 2, 0)], [(group_vals, 3, 0)], [], sig_unit(0, 0), sig_unit(0, 1), [], sig_unit(1, 0), sig_unit(1, 1)]
+        scalar = [(group_vals, 1, 0)]
         for n in range(8):
             scalar += [(group_keys, 2 * n), (group_keys, 2 * n + 1)] + extras[n]
-        scalar += sig_unit(2, 0) + sig_unit(3, 0) + [(group_vals, 3, 0)] + sig_unit(2, 1) + [(group_vals, 0, 1), (group_vals, 1, 1)] + sig_unit(3, 1)
-        scalar += [(group_vals, G, 1) for G in range(2, 4)]
-        pairs = [(0, 0), (1, 0), (0, 1), (1, 1), (2, 0), (3, 0), (2, 1), (3, 1)]
-        for i in range(9):
-            if i == 4:
-                scalar += [(group_y, *pairs[i - 1])]
-            if i < 8:
-                scalar += rounds(*pairs[i])
-            if i > 0 and i != 4:
-                scalar += [(group_y, *pairs[i - 1])]
+        scalar += sig_unit(2, 0) + sig_unit(3, 0) + [(group_vals, G, 1) for G in range(4)]
+        scalar += sig_unit(2, 1) + rounds(0, 0) + sig_unit(3, 1) + rounds(1, 0) + [(group_y, 0, 0)]
+        scalar += rounds(0, 1) + [(group_y, 1, 0)] + rounds(1, 1) + [(group_y, 0, 1), (group_y, 1, 1)]
+        scalar += rounds(2, 0) + rounds(3, 0) + [(group_y, 2, 0)] + rounds(2, 1) + [(group_y, 3, 0), (group_y, 2, 1), (group_y, 3, 1)]
 
         tensor = []
         for n in range(8):
             tensor += [(turn_keys, 2 * n), (turn_keys, 2 * n + 1)] + [(logits, *s[1:]) for s in extras[n] if s[0] is sigmoid]
-        tensor += logit_unit(2, 0) + logit_unit(3, 0) + logit_unit(2, 1)[:2] + mixes(A, [0, 1]) + logit_unit(2, 1)[2:]
-        tensor += mixes(A, [2]) + logit_unit(3, 1)[:3] + mixes(A, [3]) + logit_unit(3, 1)[3:]
-        tensor += mixes(B, [0, 1]) + mixes(C[:2], [0]) + mixes(B, [2, 3]) + mixes(C[:2], [1]) + turns(A)
-        tensor += mixes(C[2:], [0, 1]) + mixes(C, [2]) + mixes(E[:2], [0, 1, 2]) + turns(B)
-        tensor += mixes(C, [3]) + mixes(E[:2], [3])
+        tensor += logit_unit(2, 0) + logit_unit(3, 0) + logit_unit(2, 1)[:3] + mixes(A, range(4))
+        tensor += mixes(B, [0, 1]) + logit_unit(2, 1)[3:] + logit_unit(3, 1)[:2] + mixes(B, [2]) + logit_unit(3, 1)[2:3]
+        tensor += mixes(B, [3]) + logit_unit(3, 1)[3:] + turns(A[:2])
+        tensor += mixes(C[:2], [0]) + turns(A[2:]) + mixes(C[2:] + E[:2], [0]) + mixes(C + E[:2], [1]) + turns(B)
+        tensor += mixes(C + E[:2], [2])
+        tensor += mixes(C + E[:2], [3])
         tensor += mixes(E[2:3], range(4)) + turns(C[:2]) + mixes(E[3:], range(4)) + turns(C[2:]) + turns(E)
 
 
-        queues = [vector, scalar, tensor]
+        queues = [scalar, vector, tensor]
         done = set()
         while any(queues):
             moved = False

@@ -17,7 +17,14 @@ MULT = mybir.AluOpType.mult
 SIGMOID = mybir.ActivationFunctionType.Sigmoid
 
 P = 128
+PACK = 4
 W = 512
+GROUPS = S // W
+SLABS = GROUPS * PACK
+PAIRS = SLABS // 2
+KEY_TILES = 4
+GATE_TILES = 3
+QUANTIZE_LAG = 2
 
 
 def tile_gated_sigmoid_attention_b7_kernel(
@@ -25,66 +32,113 @@ def tile_gated_sigmoid_attention_b7_kernel(
 ):
     nc = tc.nc
     with ExitStack() as ctx:
-        keep = ctx.enter_context(tc.tile_pool(name="keep", bufs=1))
-        work = ctx.enter_context(tc.tile_pool(name="work", bufs=2))
+        sbuf = ctx.enter_context(tc.tile_pool(name="sbuf", bufs=1))
         psum = ctx.enter_context(tc.psum_pool(name="psum", bufs=1))
         ctx.enter_context(tc.manual_schedule())
 
-        def bank(i):
-            return psum.tile([P, W], F32, name="bank%d" % i)
+        def sbuf_tile(name, width, dtype):
+            return sbuf.tile([P, width], dtype, name=name, align_bytes=64)
 
-        def kept(name, width, dtype):
-            return keep.tile([P, width], dtype, name=name, align_bytes=64)
+        def psum_bank(number):
+            return psum.tile([P, W], F32, name="bank%d" % number)
 
-        def passing(name, width, dtype, bufs):
-            return work.tile([P, width], dtype, name=name, bufs=bufs, align_bytes=64)
+        free = {
+            "key_wide": [0, 1, 2, 3],
+            "key_grouped": [0, 1, 2],
+            "val_grouped": [0, 1, 2, 3],
+            "sigmoid": [0, 1, 2, 3, 4, 5],
+            "att_grouped": [0, 1],
+            "y": [0, 1, 2, 3, 4, 5, 6, 7],
+            "y_rounded": [0, 1, 2, 3],
+            "y_grouped": [0, 1, 2],
+            "y_codes": [0, 1, 2, 3],
+            "logit_bank": [0, 1, 2],
+            "key_bank": [3, 4, 5, 6],
+            "y_bank": [7],
+            "sum_bank": [],
+        }
+        key_banks, logit_banks = len(free["key_bank"]), len(free["logit_bank"])
+        held, slot_of = {}, {}
+
+        def take(kind, key, width=W, dtype=F32):
+            slot = free[kind][0]
+            free[kind].remove(slot)
+            slot_of[kind, key] = slot
+            held[kind, key] = psum_bank(slot) if "bank" in kind else sbuf_tile("%s%d" % (kind, slot), width, dtype)
+            return held[kind, key]
+
+        def give(kind, key, to=None):
+            free[to or kind].append(slot_of[kind, key])
 
         def quantize(name, grouped):
-            width = grouped.shape[1] // 4
-            codes = kept(name + "_codes", width, U32)
-            scales = kept(name + "_scales", width, U8)
+            width = grouped.shape[1] // PACK
+            codes = sbuf_tile(name + "_codes", width, U32)
+            scales = sbuf_tile(name + "_scales", width, U8)
             nc.vector.quantize_mx(out=codes[:].bitcast(FP8X4), scales=scales[:], in_=grouped[:])
             return codes, scales
 
-        key_rows = keys_bytes.rearrange("(G m a j) k -> G a m (j k)", m=P, a=2, j=2)
-        key_tiles, val_raw, gate_tiles, q_codes = {}, {}, {}, {}
+        def as_planes(ap):
+            return ap.rearrange("p (t c i) -> p c t i", i=4, t=PACK)
+
+        def as_grouped(ap):
+            return ap.rearrange("p (c i t) -> p c t i", i=4, t=PACK)
+
+        key_bytes, val_planes, gate_tiles, query_codes = {}, {}, {}, {}
 
         def load_keys(n):
-            key_tiles[n] = work.tile([P, 2 * D], U8, name="key_bytes%d" % (n % 6), bufs=1)
-            nc.sync.dma_start(out=key_tiles[n][:], in_=key_rows[n // 2, n % 2])
+            key_bytes[n] = sbuf_tile("key_bytes%d" % (n % KEY_TILES), 2 * D, U8)
+            rows = keys_bytes.rearrange("(G m a t) k -> G a m (t k)", m=P, a=2, t=2)
+            nc.sync.dma_start(out=key_bytes[n][:], in_=rows[n // 2, n % 2])
 
-        def load_vals(G, h):
-            val_raw[G, h] = work.tile([P, 4 * W], BF16, name="val_raw%d" % G, bufs=1)
+        def load_val_columns(planes, G, first, width):
             nc.sync.dma_start(
-                out=val_raw[G, h][:].rearrange("p (t w) -> p t w", t=4),
-                in_=vals[G * W : (G + 1) * W, h * W : (h + 1) * W].rearrange("(p t) w -> p t w", t=4),
+                out=planes.rearrange("p (t w) -> p t w", t=PACK),
+                in_=vals[G * W : (G + 1) * W, first : first + width].rearrange("(p t) w -> p t w", t=PACK),
             )
 
+        def load_vals(G, h):
+            val_planes[G, h] = sbuf_tile("val_planes%d" % G, PACK * W, BF16)
+            load_val_columns(val_planes[G, h][:], G, h * W, W)
+
         def load_gate(b, h):
-            gate_tiles[b, h] = work.tile([P, 4 * W], BF16, name="gate%d" % ((2 * b + h) % 3), bufs=1)
+            gate_tiles[b, h] = sbuf_tile("gate%d" % ((2 * b + h) % GATE_TILES), 4 * W, BF16)
             nc.sync.dma_start(
                 out=gate_tiles[b, h][:].rearrange("p (j w) -> p j w", j=4),
                 in_=gate[b * W : (b + 1) * W, h * W : (h + 1) * W].rearrange("(j p) w -> p j w", p=P),
             )
 
         def load_queries(b):
-            q_codes[b] = kept("q_codes%d" % b, 2 * W, U32)
+            query_codes[b] = sbuf_tile("query_codes%d" % b, 2 * W, U32)
+            words = qry_words.rearrange("g p n t -> p g (n t)")[:, :, b * PACK * W : (b + 1) * PACK * W]
             nc.sync.dma_start(
-                out=q_codes[b][:].bitcast(I32).rearrange("p (g n) -> p g n", g=2),
-                in_=qry_words.rearrange("g p n t -> p g (n t)")[:, :, b * 4 * W : (b + 1) * 4 * W].bitcast(I32),
+                out=query_codes[b][:].bitcast(I32).rearrange("p (g n) -> p g n", g=2), in_=words.bitcast(I32)
             )
 
-        scale_cols = kept("scale_cols", 8, F32)
-        nc.sync.dma_start(out=scale_cols[:], in_=keys_scale.rearrange("o (p c) -> p (o c)", c=8))
-        ident = kept("ident", P, F32)
-        make_identity(nc, ident[:])
-        q_scales = kept("q_scales", 2 * T, U8)
-        nc.gpsimd.memset(q_scales[:].bitcast(I32), 0)
-        warm = kept("warm", 1, F32)
-        nc.scalar.activation(out=warm[:], in_=ident[:, 0:1], func=SIGMOID)
+        def load_per_key(name, row):
+            columns = sbuf_tile(name, SLABS, BF16)
+            nc.sync.dma_start(
+                out=columns[:].rearrange("m (G t) -> m G t", t=PACK),
+                in_=row.rearrange("o (G m t) -> m (o G) t", m=P, t=PACK),
+            )
+            return columns
 
-        load_vals(0, 0)
+        scale_columns = sbuf_tile("scale_columns", 8, F32)
+        nc.sync.dma_start(
+            out=scale_columns[:].rearrange("p (g c) -> p g c", c=4),
+            in_=keys_scale.rearrange("o (g p c) -> p (o g) c", p=P, c=4),
+        )
+        identity = sbuf_tile("identity", P, F32)
+        make_identity(nc, identity[:])
+        query_scales = sbuf_tile("query_scales", 2 * T, U8)
+        nc.gpsimd.memset(query_scales[:].bitcast(I32), 0)
+        warm_up = sbuf_tile("warm_up", 1, F32)
+        nc.scalar.activation(out=warm_up[:], in_=identity[:, 0:1], func=SIGMOID)
+
+        first_planes = sbuf_tile("val_planes0", PACK * W, BF16)
+        piece = [slice(0, 2 * W), slice(2 * W, 4 * W)]
+        load_val_columns(first_planes[:, piece[0]], 0, 0, W // 2)
         load_keys(0)
+        load_val_columns(first_planes[:, piece[1]], 0, W // 2, W // 2)
         load_vals(1, 0)
         load_keys(1)
         load_keys(2)
@@ -94,345 +148,284 @@ def tile_gated_sigmoid_attention_b7_kernel(
         load_queries(0)
         for Q in range(4):
             nc.sync.dma_start(
-                out=q_scales[32 * Q : 32 * Q + 4, :].bitcast(I32).rearrange("r (g n) -> r g n", g=2),
+                out=query_scales[32 * Q : 32 * Q + 4, :].bitcast(I32).rearrange("r (g n) -> r g n", g=2),
                 in_=qry_scales[:, 4 * Q : 4 * Q + 4, :].rearrange("g r n -> r g n").bitcast(I32),
             )
-        bias = kept("bias", 16, BF16)
-        gain = kept("gain", 16, BF16)
-        nc.sync.dma_start(
-            out=bias[:].rearrange("m (G t) -> m G t", t=4), in_=key_bias.rearrange("o (G m t) -> m (o G) t", m=P, t=4)
-        )
-        nc.sync.dma_start(
-            out=gain[:].rearrange("m (G t) -> m G t", t=4), in_=key_gain.rearrange("o (G m t) -> m (o G) t", m=P, t=4)
-        )
-        load_keys(4)
-        load_keys(5)
-        load_queries(1)
+        bias = load_per_key("bias", key_bias)
+        gain = load_per_key("gain", key_gain)
 
-        scale_all = kept("scale_all", D, F32)
-        for half in range(2):
-            spread = bank(half)
+        scale_rows = sbuf_tile("scale_rows", D, F32)
+        for g in range(2):
+            spread = psum_bank(g)
             for c in range(4):
-                col = 4 * half + c
-                nc.tensor.transpose(
-                    spread[:, c * P : (c + 1) * P], scale_cols[:, col : col + 1].to_broadcast([P, P]), ident[:]
-                )
-            dst = scale_all[:].rearrange("q (p c) -> q p c", c=8)[:, :, 4 * half : 4 * half + 4]
-            src = spread[:].rearrange("q (c p) -> q p c", c=4)
-            nc.scalar.copy(out=dst, in_=src)
-
-        tiles = {}
-        y_scales = kept("y_scales", 2 * T, U8)
-        free = {
-            "key_wide": [0, 1, 2, 3],
-            "key_grouped": [0, 1, 2],
-            "val_grouped": [0, 1, 2, 3],
-            "sig": [0, 1, 2, 3, 4, 5],
-            "att_grouped": [0, 1],
-            "y": [0, 1, 2, 3, 4, 5],
-            "y_rounded": [0, 1, 2, 3],
-            "y_grouped": [0, 1, 2],
-            "logit_bank": [0, 1, 2],
-            "key_bank": [3, 4, 5, 6],
-            "sum_bank": [],
-            "y_bank": [7],
-        }
-        slot_of = {}
-
-        def take(kind, key, width=W, dtype=F32):
-            slot = free[kind][0]
-            free[kind].remove(slot)
-            slot_of[kind, key] = slot
-            if "bank" in kind:
-                tiles[kind, key] = bank(slot)
-            else:
-                tiles[kind, key] = work.tile([P, width], dtype, name="%s%d" % (kind, slot), bufs=1, align_bytes=64)
-            return tiles[kind, key]
-
-        def give(kind, key, to=None):
-            free[to or kind].append(slot_of[kind, key])
-
-        key_q, val_q, att_q = {}, {}, {}
-
-        def widen_keys(i):
-            wide = take("key_wide", i, D, BF16)
-            nc.vector.tensor_tensor(
-                out=wide[:], in0=key_tiles[i // 2][:, (i % 2) * D : (i % 2 + 1) * D].bitcast(FP8), in1=scale_all[:], op=MULT
+                column = scale_columns[:, 4 * g + c : 4 * g + c + 1]
+                nc.tensor.transpose(spread[:, c * P : (c + 1) * P], column.to_broadcast([P, P]), identity[:])
+            nc.scalar.copy(
+                out=scale_rows[:, g * W : (g + 1) * W].rearrange("q (p c) -> q p c", c=4),
+                in_=spread[:].rearrange("q (c p) -> q p c", c=4),
             )
-            if i in (1, 3):
-                load_keys(6 + i // 2)
 
-        def turn_keys(i):
-            words = tiles["key_wide", i][:].bitcast(F32)
-            turned = take("key_bank", i)
+        first_grouped = take("val_grouped", (0, 0), PACK * W, BF16)
+        nc.vector.tensor_copy(out=as_grouped(first_grouped[:, piece[0]]), in_=as_planes(first_planes[:, piece[0]]))
+        nc.scalar.copy(out=as_grouped(first_grouped[:, piece[1]]), in_=as_planes(first_planes[:, piece[1]]))
+
+        key_mx, val_mx, att_mx = {}, {}, {}
+        y_scales = sbuf_tile("y_scales", 2 * T, U8)
+
+        def widen_keys(slab):
+            wide = take("key_wide", slab, D, BF16)
+            values = key_bytes[slab // 2][:, (slab % 2) * D : (slab % 2 + 1) * D].bitcast(FP8)
+            for cols in [slice(0, W), slice(W, D)] if slab == 0 else [slice(0, D)]:
+                nc.vector.tensor_tensor(out=wide[:, cols], in0=values[:, cols], in1=scale_rows[:, cols], op=MULT)
+
+        def turn_keys(slab):
+            words = held["key_wide", slab][:].bitcast(F32)
+            bank = take("key_bank", slab)
             for g in range(2):
                 for u in range(2):
                     c = 2 * g + u
                     nc.tensor.transpose(
-                        turned[:, c * P : (c + 1) * P], words[:, 256 * g + u : 256 * (g + 1) : 2], ident[:]
+                        bank[:, c * P : (c + 1) * P], words[:, 2 * P * g + u : 2 * P * (g + 1) : 2], identity[:]
                     )
-            give("key_wide", i)
+            give("key_wide", slab)
 
-        def group_keys(i):
-            n, j = divmod(i, 2)
-            if j == 0:
+        def group_keys(slab):
+            n, second = divmod(slab, 2)
+            if not second:
                 take("key_grouped", n, 2 * D, BF16)
+            words = held["key_grouped", n][:].bitcast(F32)[:, second * W : (second + 1) * W]
             nc.scalar.copy(
-                out=tiles["key_grouped", n][:].bitcast(F32)[:, j * W : (j + 1) * W].rearrange("p (g m u) -> p g m u", g=2, u=2),
-                in_=tiles["key_bank", i][:].rearrange("p (g u m) -> p g m u", g=2, u=2),
+                out=words.rearrange("p (g m u) -> p g m u", g=2, u=2),
+                in_=held["key_bank", slab][:].rearrange("p (g u m) -> p g m u", g=2, u=2),
             )
-            give("key_bank", i, "sum_bank" if i >= 12 else None)
+            give("key_bank", slab, "sum_bank" if slab >= SLABS - key_banks else None)
 
         def quantize_keys(n):
-            key_q[n] = quantize("key%d" % n, tiles["key_grouped", n])
+            key_mx[n] = quantize("key%d" % n, held["key_grouped", n])
             give("key_grouped", n)
 
         def group_vals(G, h):
-            grouped = take("val_grouped", (G, h), 4 * W, BF16)
-            dst = grouped[:].rearrange("p (c i t) -> p c t i", i=4, t=4)
-            src = val_raw[G, h][:].rearrange("p (t c i) -> p c t i", i=4, t=4)
-            if (G, h) == (0, 0):
-                nc.vector.tensor_copy(out=dst, in_=src)
-            else:
-                nc.scalar.copy(out=dst, in_=src)
-            if h == 0:
-                load_vals(G, 1)
-            if (G, h) == (3, 0):
-                load_gate(0, 0)
-                load_gate(0, 1)
-                load_gate(1, 0)
+            grouped = take("val_grouped", (G, h), PACK * W, BF16)
+            nc.scalar.copy(out=as_grouped(grouped[:]), in_=as_planes(val_planes[G, h][:]))
 
         def quantize_vals(G, h):
-            val_q[G, h] = quantize("val%d_%d" % (G, h), tiles["val_grouped", (G, h)])
+            val_mx[G, h] = quantize("val%d_%d" % (G, h), held["val_grouped", (G, h)])
             give("val_grouped", (G, h))
 
         def logits(G, b, t):
-            codes, scales = key_q[2 * G + t // 2]
-            out = take("logit_bank", (G, b, t))
+            codes, scales = key_mx[2 * G + t // 2]
+            bank = take("logit_bank", (G, b, t))
             for g in range(2):
-                cols = slice((t % 2) * 256 + g * P, (t % 2) * 256 + (g + 1) * P)
+                keys = slice((2 * (t % 2) + g) * P, (2 * (t % 2) + g + 1) * P)
                 nc.tensor.matmul_mx(
-                    out=out[:],
-                    lhsT=codes[:, cols].bitcast(FP8X4),
-                    lhsT_scale=scales[:, cols],
-                    rhs=q_codes[b][:, g * W : (g + 1) * W].bitcast(FP8X4),
-                    rhs_scale=q_scales[:, g * T + b * W : g * T + (b + 1) * W],
+                    out=bank[:],
+                    lhsT=codes[:, keys].bitcast(FP8X4),
+                    lhsT_scale=scales[:, keys],
+                    rhs=query_codes[b][:, g * W : (g + 1) * W].bitcast(FP8X4),
+                    rhs_scale=query_scales[:, g * T + b * W : g * T + (b + 1) * W],
                     start=(g == 0),
                     stop=(g == 1),
                 )
 
         def sigmoid(G, b, t):
             if t == 0:
-                take("sig", (G, b), 4 * W, F32)
+                take("sigmoid", (G, b), PACK * W, F32)
             nc.scalar.activation(
-                out=tiles["sig", (G, b)][:, t * W : (t + 1) * W],
-                in_=tiles["logit_bank", (G, b, t)][:],
+                out=held["sigmoid", (G, b)][:, t * W : (t + 1) * W],
+                in_=held["logit_bank", (G, b, t)][:],
                 func=SIGMOID,
-                bias=bias[:, 4 * G + t : 4 * G + t + 1],
+                bias=bias[:, PACK * G + t : PACK * G + t + 1],
             )
-            last = (G, b) == (3, 1) and t >= 1
-            give("logit_bank", (G, b, t), ("y_bank" if t == 1 else "sum_bank") if last else None)
+            retired = t - (PACK - logit_banks) if (G, b) == (GROUPS - 1, 1) else -1
+            give("logit_bank", (G, b, t), None if retired < 0 else "y_bank" if retired == 0 else "sum_bank")
 
         def apply_gain(G, b):
-            grouped = take("att_grouped", (G, b), 4 * W, BF16)
+            grouped = take("att_grouped", (G, b), PACK * W, BF16)
+            gains = gain[:, PACK * G : PACK * (G + 1)].unsqueeze(1).unsqueeze(3)
             nc.vector.tensor_tensor(
-                out=grouped[:].rearrange("p (c i t) -> p c t i", i=4, t=4),
-                in0=tiles["sig", (G, b)][:].rearrange("p (t c i) -> p c t i", i=4, t=4),
-                in1=gain[:, 4 * G : 4 * G + 4].unsqueeze(1).unsqueeze(3).to_broadcast([P, W // 4, 4, 4]),
+                out=as_grouped(grouped[:]),
+                in0=as_planes(held["sigmoid", (G, b)][:]),
+                in1=gains.to_broadcast([P, W // 4, PACK, 4]),
                 op=MULT,
             )
-            give("sig", (G, b))
+            give("sigmoid", (G, b))
 
         def quantize_att(G, b):
-            att_q[G, b] = quantize("att%d_%d" % (G, b), tiles["att_grouped", (G, b)])
+            att_mx[G, b] = quantize("att%d_%d" % (G, b), held["att_grouped", (G, b)])
             give("att_grouped", (G, b))
 
         def mix(j, h, G):
             if G == 0:
                 take("sum_bank", (j, h))
-            codes, scales = att_q[G, j // 4]
-            cols = slice((j % 4) * P, (j % 4 + 1) * P)
+            att_codes, att_scales = att_mx[G, j // 4]
+            val_codes, val_scales = val_mx[G, h]
+            queries = slice((j % 4) * P, (j % 4 + 1) * P)
             nc.tensor.matmul_mx(
-                out=tiles["sum_bank", (j, h)][:],
-                lhsT=codes[:, cols].bitcast(FP8X4),
-                lhsT_scale=scales[:, cols],
-                rhs=val_q[G, h][0][:].bitcast(FP8X4),
-                rhs_scale=val_q[G, h][1][:],
+                out=held["sum_bank", (j, h)][:],
+                lhsT=att_codes[:, queries].bitcast(FP8X4),
+                lhsT_scale=att_scales[:, queries],
+                rhs=val_codes[:].bitcast(FP8X4),
+                rhs_scale=val_scales[:],
                 start=(G == 0),
-                stop=(G == 3),
+                stop=(G == GROUPS - 1),
             )
 
         def apply_gate(j, h):
             y = take("y", (j, h))
             nc.vector.tensor_tensor(
                 out=y[:],
-                in0=tiles["sum_bank", (j, h)][:],
+                in0=held["sum_bank", (j, h)][:],
                 in1=gate_tiles[j // 4, h][:, (j % 4) * W : (j % 4 + 1) * W],
                 op=MULT,
             )
             give("sum_bank", (j, h))
             nc.sync.dma_start(out=out_0[j * P : (j + 1) * P, h * W : (h + 1) * W], in_=y[:])
-            if (j, h) == (3, 0):
-                load_gate(1, 1)
 
-        def round_y(j, h, engine):
+        def round_y(j, h):
             rounded = take("y_rounded", (j, h), W, BF16)
-            dst = rounded[:].rearrange("p (u m e) -> p u m e", u=2, e=2)
-            src = tiles["y", (j, h)][:].rearrange("p (m u e) -> p u m e", u=2, e=2)
-            if engine == "V":
-                nc.vector.tensor_copy(out=dst, in_=src)
-            else:
-                nc.scalar.copy(out=dst, in_=src)
+            cast = nc.vector.tensor_copy if (j, h) in last_pair else nc.scalar.copy
+            cast(
+                out=rounded[:].rearrange("p (u m e) -> p u m e", u=2, e=2),
+                in_=held["y", (j, h)][:].rearrange("p (m u e) -> p u m e", u=2, e=2),
+            )
             give("y", (j, h))
 
         def turn_y(j, h):
             if j % 2 == 0:
                 take("y_bank", (j // 2, h))
-            words = tiles["y_rounded", (j, h)][:].bitcast(F32)
+            words = held["y_rounded", (j, h)][:].bitcast(F32)
             for u in range(2):
                 c = 2 * (j % 2) + u
                 nc.tensor.transpose(
-                    tiles["y_bank", (j // 2, h)][:, c * P : (c + 1) * P], words[:, u * P : (u + 1) * P], ident[:]
+                    held["y_bank", (j // 2, h)][:, c * P : (c + 1) * P], words[:, u * P : (u + 1) * P], identity[:]
                 )
             give("y_rounded", (j, h))
 
-        def group_y(pair, h):
-            grouped = take("y_grouped", (pair, h), 2 * W, BF16)
+        def group_y(r, h):
+            grouped = take("y_grouped", (r, h), 2 * W, BF16)
             nc.scalar.copy(
-                out=grouped[:].bitcast(F32).rearrange("p (j r u) -> p j r u", j=2, u=2),
-                in_=tiles["y_bank", (pair, h)][:].rearrange("p (j u r) -> p j r u", j=2, u=2),
+                out=grouped[:].bitcast(F32).rearrange("p (j m u) -> p j m u", j=2, u=2),
+                in_=held["y_bank", (r, h)][:].rearrange("p (j u m) -> p j m u", j=2, u=2),
             )
-            give("y_bank", (pair, h))
+            give("y_bank", (r, h))
 
-        def quantize_y(pair, h):
-            codes = passing("y_codes", 2 * P, U32, 4)
-            cols = slice(h * T + pair * 2 * P, h * T + (pair + 1) * 2 * P)
+        def quantize_y(r, h):
+            codes = take("y_codes", (r, h), 2 * P, U32)
             nc.vector.quantize_mx(
-                out=codes[:].bitcast(FP8X4), scales=y_scales[:, cols], in_=tiles["y_grouped", (pair, h)][:]
+                out=codes[:].bitcast(FP8X4),
+                scales=y_scales[:, h * T + r * 2 * P : h * T + (r + 1) * 2 * P],
+                in_=held["y_grouped", (r, h)][:],
             )
-            give("y_grouped", (pair, h))
-            nc.sync.dma_start(
-                out=out_1[h].rearrange("p m t -> p (m t)")[:, pair * 8 * P : (pair + 1) * 8 * P].bitcast(I32),
-                in_=codes[:].bitcast(I32),
-            )
+            give("y_grouped", (r, h))
+            words = out_1[h].rearrange("p m t -> p (m t)")[:, r * 2 * P * PACK : (r + 1) * 2 * P * PACK]
+            nc.sync.dma_start(out=words.bitcast(I32), in_=codes[:].bitcast(I32))
+            give("y_codes", (r, h))
 
-        def needs(step):
-            fn, a = step[0], step[1:]
-            if fn is widen_keys:
-                return [], "key_wide"
-            if fn is turn_keys:
-                return [(widen_keys, *a)], "key_bank"
-            if fn is group_keys:
-                return [(turn_keys, *a)], ("key_grouped" if a[0] % 2 == 0 else None)
-            if fn is quantize_keys:
-                return [(group_keys, 2 * a[0] + 1)], None
-            if fn is group_vals:
-                return [], "val_grouped"
-            if fn is quantize_vals:
-                return [(group_vals, *a)], None
-            if fn is logits:
-                return [(quantize_keys, 2 * a[0] + a[2] // 2)], "logit_bank"
-            if fn is sigmoid:
-                return [(logits, *a)], ("sig" if a[2] == 0 else None)
-            if fn is apply_gain:
-                return [(sigmoid, *a, 3)], "att_grouped"
-            if fn is quantize_att:
-                return [(apply_gain, *a)], None
-            if fn is mix:
-                return [(quantize_att, a[2], a[0] // 4), (quantize_vals, a[2], a[1])], ("sum_bank" if a[2] == 0 else None)
-            if fn is apply_gate:
-                return [(mix, *a, 3)], "y"
-            if fn is round_y:
-                return [(apply_gate, a[0], a[1])], "y_rounded"
-            if fn is turn_y:
-                return [(round_y, *a, round_engine(*a))], ("y_bank" if a[0] % 2 == 0 else None)
-            if fn is group_y:
-                return [(turn_y, 2 * a[0] + 1, a[1])], "y_grouped"
-            return [(group_y, *a)], None
+        before = {
+            load_keys: lambda n: ([(widen_keys, 2 * (n - KEY_TILES) + 1)], None),
+            load_vals: lambda G, h: ([(group_vals, G, 0)], None),
+            load_queries: lambda b: ([], None),
+            load_gate: lambda b, h: ([(apply_gate, 3, 0)] if (b, h) == (1, 1) else [], None),
+            widen_keys: lambda slab: ([(load_keys, slab // 2)], "key_wide"),
+            turn_keys: lambda slab: ([(widen_keys, slab)], "key_bank"),
+            group_keys: lambda slab: ([(turn_keys, slab)], None if slab % 2 else "key_grouped"),
+            quantize_keys: lambda n: ([(group_keys, 2 * n + 1)], None),
+            group_vals: lambda G, h: ([(load_vals, G, h)], "val_grouped"),
+            quantize_vals: lambda G, h: ([(group_vals, G, h)], None),
+            logits: lambda G, b, t: ([(quantize_keys, 2 * G + t // 2), (load_queries, b)], "logit_bank"),
+            sigmoid: lambda G, b, t: ([(logits, G, b, t)], None if t else "sigmoid"),
+            apply_gain: lambda G, b: ([(sigmoid, G, b, PACK - 1)], "att_grouped"),
+            quantize_att: lambda G, b: ([(apply_gain, G, b)], None),
+            mix: lambda j, h, G: ([(quantize_att, G, j // 4), (quantize_vals, G, h)], None if G else "sum_bank"),
+            apply_gate: lambda j, h: ([(mix, j, h, GROUPS - 1), (load_gate, j // 4, h)], "y"),
+            round_y: lambda j, h: ([(apply_gate, j, h)], "y_rounded"),
+            turn_y: lambda j, h: ([(round_y, j, h)], None if j % 2 else "y_bank"),
+            group_y: lambda r, h: ([(turn_y, 2 * r + 1, h)], "y_grouped"),
+            quantize_y: lambda r, h: ([(group_y, r, h)], "y_codes"),
+        }
+        done = {(load_keys, n) for n in range(KEY_TILES)} | {(load_vals, G, 0) for G in range(GROUPS)}
+        done = done | {(load_queries, 0), (group_vals, 0, 0)}
 
-        def round_engine(j, h):
-            return "V" if (h == 1 and j >= 6) else "S"
+        def each(step, arguments):
+            return [(step, *a) for a in arguments]
 
-        def sig_unit(G, b):
-            return [(sigmoid, G, b, t) for t in range(4)]
+        def slabs_of(G, b):
+            return [(G, b, t) for t in range(PACK)]
 
-        def logit_unit(G, b):
-            return [(logits, G, b, t) for t in range(4)]
+        def passes(units, groups):
+            return [(mix, j, h, G) for G in groups for j, h in units]
 
-        def rounds(pair, h):
-            return [(round_y, j, h, "S") for j in (2 * pair, 2 * pair + 1) if round_engine(j, h) == "S"]
+        set_a, set_b, set_c, set_d = [[(4 * b + j, h) for j in range(4)] for b in range(2) for h in range(2)]
+        last_pair = set_d[2:]
 
-        A = [(j, 0) for j in range(4)]
-        B = [(j, 1) for j in range(4)]
-        C = [(j, 0) for j in range(4, 8)]
-        E = [(j, 1) for j in range(4, 8)]
-
-        def gates(units):
-            return [(apply_gate, j, h) for j, h in units]
-
-        def mixes(units, Gs):
-            return [(mix, j, h, G) for G in Gs for j, h in units]
-
-        def turns(units):
-            return [(turn_y, j, h) for j, h in units]
+        loads = [(load_keys, 4), (load_keys, 5), (load_queries, 1), (load_keys, 6), (load_keys, 7)]
+        loads += [(load_vals, G, 1) for G in range(GROUPS)]
+        loads += each(load_gate, [(0, 0), (0, 1), (1, 0), (1, 1)])
 
         vector = []
-        vector += [(group_vals, 0, 0)]
-        for n in range(8):
+        for n in range(PAIRS):
             vector += [(widen_keys, 2 * n), (widen_keys, 2 * n + 1)]
-            if n >= 2:
-                vector += [(quantize_keys, n - 2)]
-        vector += [(quantize_keys, 6), (apply_gain, 0, 0), (quantize_vals, 0, 0), (quantize_keys, 7), (quantize_att, 0, 0)]
-        for G in range(1, 4):
+            if n >= QUANTIZE_LAG:
+                vector += [(quantize_keys, n - QUANTIZE_LAG)]
+        vector += [(apply_gain, 0, 0), (quantize_keys, PAIRS - 2), (quantize_vals, 0, 0), (quantize_keys, PAIRS - 1)]
+        vector += [(quantize_att, 0, 0)]
+        for G in range(1, GROUPS):
             vector += [(apply_gain, G, 0), (quantize_vals, G, 0), (quantize_att, G, 0)]
-        vector += [(quantize_vals, 0, 1), (quantize_vals, 1, 1)] + gates(A)
-        vector += [(apply_gain, 0, 1), (quantize_vals, 2, 1), (quantize_vals, 3, 1), (quantize_att, 0, 1)]
-        vector += [(apply_gain, 1, 1)] + gates(B[:2]) + [(quantize_att, 1, 1)] + gates(B[2:])
-        vector += [(apply_gain, 2, 1), (quantize_y, 0, 0), (quantize_att, 2, 1), (quantize_y, 1, 0)]
-        vector += [(apply_gain, 3, 1), (quantize_y, 0, 1), (quantize_att, 3, 1), (quantize_y, 1, 1)]
-        vector += gates(C) + gates(E) + [(round_y, 6, 1, "V"), (round_y, 7, 1, "V")]
-        vector += [(quantize_y, 2, 0), (quantize_y, 3, 0), (quantize_y, 2, 1), (quantize_y, 3, 1)]
+        vector += [(quantize_vals, 0, 1)] + each(apply_gate, set_a) + [(quantize_vals, 1, 1), (quantize_vals, 2, 1)]
+        vector += [(apply_gain, 0, 1), (quantize_vals, 3, 1), (quantize_att, 0, 1)]
+        vector += [(apply_gain, 1, 1)] + each(apply_gate, set_b[:2]) + [(quantize_att, 1, 1)]
+        vector += each(apply_gate, set_b[2:])
+        vector += [(apply_gain, 2, 1), (quantize_y, 0, 0), (quantize_att, 2, 1)]
+        vector += [(apply_gain, 3, 1), (quantize_y, 1, 0), (quantize_att, 3, 1), (quantize_y, 0, 1), (quantize_y, 1, 1)]
+        vector += each(apply_gate, set_c + set_d) + each(round_y, last_pair)
+        vector += each(quantize_y, [(2, 0), (3, 0), (2, 1), (3, 1)])
 
-        extras = [[(group_vals, 2, 0)], [(group_vals, 3, 0)], [], sig_unit(0, 0), sig_unit(0, 1), [], sig_unit(1, 0), sig_unit(1, 1)]
+        between = [[(group_vals, 2, 0)], [(group_vals, 3, 0)]]
+        for G in range(GROUPS - 1):
+            between += [[], each(sigmoid, slabs_of(G, 0))]
         scalar = [(group_vals, 1, 0)]
-        for n in range(8):
-            scalar += [(group_keys, 2 * n), (group_keys, 2 * n + 1)] + extras[n]
-        scalar += sig_unit(2, 0) + sig_unit(3, 0) + [(group_vals, G, 1) for G in range(4)]
-        scalar += sig_unit(2, 1) + rounds(0, 0) + sig_unit(3, 1) + rounds(1, 0) + [(group_y, 0, 0)]
-        scalar += rounds(0, 1) + [(group_y, 1, 0)] + rounds(1, 1) + [(group_y, 0, 1), (group_y, 1, 1)]
-        scalar += rounds(2, 0) + rounds(3, 0) + [(group_y, 2, 0)] + rounds(2, 1) + [(group_y, 3, 0), (group_y, 2, 1), (group_y, 3, 1)]
+        for n in range(PAIRS):
+            scalar += [(group_keys, 2 * n), (group_keys, 2 * n + 1)] + between[n]
+        early_logits = slabs_of(0, 1) + slabs_of(3, 0) + slabs_of(1, 1)
+        scalar += each(sigmoid, early_logits) + [(group_vals, G, 1) for G in range(GROUPS)]
+        scalar += each(sigmoid, slabs_of(2, 1)) + each(round_y, set_a[:2])
+        scalar += each(sigmoid, slabs_of(3, 1)) + each(round_y, set_a[2:])
+        scalar += [(group_y, 0, 0)] + each(round_y, set_b[:2]) + [(group_y, 1, 0)] + each(round_y, set_b[2:])
+        scalar += [(group_y, 0, 1), (group_y, 1, 1)]
+        scalar += each(round_y, set_c) + [(group_y, 2, 0)] + each(round_y, set_d[:2])
+        scalar += each(group_y, [(3, 0), (2, 1), (3, 1)])
 
         tensor = []
-        for n in range(8):
-            tensor += [(turn_keys, 2 * n), (turn_keys, 2 * n + 1)] + [(logits, *s[1:]) for s in extras[n] if s[0] is sigmoid]
-        tensor += logit_unit(2, 0) + logit_unit(3, 0) + logit_unit(2, 1)[:3] + mixes(A, range(4))
-        tensor += mixes(B, [0, 1]) + logit_unit(2, 1)[3:] + logit_unit(3, 1)[:2] + mixes(B, [2]) + logit_unit(3, 1)[2:3]
-        tensor += mixes(B, [3]) + logit_unit(3, 1)[3:] + turns(A[:2])
-        tensor += mixes(C[:2], [0]) + turns(A[2:]) + mixes(C[2:] + E[:2], [0]) + mixes(C + E[:2], [1]) + turns(B)
-        tensor += mixes(C + E[:2], [2])
-        tensor += mixes(C + E[:2], [3])
-        tensor += mixes(E[2:3], range(4)) + turns(C[:2]) + mixes(E[3:], range(4)) + turns(C[2:]) + turns(E)
+        for n in range(PAIRS):
+            tensor += [(turn_keys, 2 * n), (turn_keys, 2 * n + 1)]
+            tensor += [(logits, *step[1:]) for step in between[n] if step[0] is sigmoid]
+        late_logits = each(logits, slabs_of(2, 1) + slabs_of(3, 1))
+        tensor += each(logits, early_logits) + late_logits[:logit_banks] + passes(set_a, range(GROUPS))
+        tensor += passes(set_b, range(3)) + late_logits[logit_banks : 2 * logit_banks]
+        tensor += passes(set_b, [3]) + late_logits[2 * logit_banks :] + each(turn_y, set_a[:2])
+        open_units = set_c + set_d[:2]
+        tensor += passes(open_units[:2], [0]) + each(turn_y, set_a[2:]) + passes(open_units[2:], [0])
+        tensor += passes(open_units, [1]) + each(turn_y, set_b) + passes(open_units, [2, 3])
+        tensor += passes(last_pair[:1], range(GROUPS)) + each(turn_y, set_c[:2])
+        tensor += passes(last_pair[1:], range(GROUPS)) + each(turn_y, set_c[2:] + set_d)
 
-
-        queues = [scalar, vector, tensor]
-        done = set()
+        queues = [loads, scalar, vector, tensor]
         while any(queues):
-            moved = False
+            written = len(done)
             for queue in queues:
                 while queue:
-                    before, kind = needs(queue[0])
-                    if not (all(x in done for x in before) and (kind is None or free[kind])):
-                        break
                     step = queue[0]
+                    earlier, kind = before[step[0]](*step[1:])
+                    if not all(other in done for other in earlier) or (kind and not free[kind]):
+                        break
                     queue.remove(step)
                     step[0](*step[1:])
                     done.add(step)
-                    moved = True
-            assert moved, [(q[0][0], q[0][1:]) for q in queues if q]
+            assert len(done) > written
 
         for Q in range(4):
-            dma_queue = nc.sync if Q % 2 == 0 else nc.scalar
-            dma_queue.dma_start(
-                out=out_2[:, 4 * Q : 4 * Q + 4, :].rearrange("g r m -> r g m").bitcast(I32),
-                in_=y_scales[32 * Q : 32 * Q + 4, :].bitcast(I32).rearrange("r (g m) -> r g m", g=2),
+            engine = nc.sync if Q % 2 == 0 else nc.scalar
+            engine.dma_start(
+                out=out_2[:, 4 * Q : 4 * Q + 4, :].rearrange("h r m -> r h m").bitcast(I32),
+                in_=y_scales[32 * Q : 32 * Q + 4, :].bitcast(I32).rearrange("r (h m) -> r h m", h=2),
             )

from contextlib import ExitStack

import concourse.mybir as mybir
from concourse.masks import make_identity

T, S, D, DV = 1024, 2048, 1024, 1024
FLOPS = 2 * T * S * D + 2 * T * S * DV

F32 = mybir.dt.float32
BF16 = mybir.dt.bfloat16
U32 = mybir.dt.uint32
I32 = mybir.dt.int32
U8 = mybir.dt.uint8
FP8 = mybir.dt.float8_e4m3fn
FP8X4 = mybir.dt.float8_e4m3fn_x4
MULT = mybir.AluOpType.mult
SIGMOID = mybir.ActivationFunctionType.Sigmoid

P = 128
PACK = 4
W = 512
GROUPS = S // W
SLABS = GROUPS * PACK
PAIRS = SLABS // 2
KEY_TILES = 4
GATE_TILES = 3
QUANTIZE_LAG = 2


def tile_gated_sigmoid_attention_b7_kernel(
    tc, qry_words, qry_scales, keys_bytes, keys_scale, key_bias, key_gain, vals, gate, out_0, out_1, out_2
):
    nc = tc.nc
    with ExitStack() as ctx:
        sbuf = ctx.enter_context(tc.tile_pool(name="sbuf", bufs=1))
        psum = ctx.enter_context(tc.psum_pool(name="psum", bufs=1))
        ctx.enter_context(tc.manual_schedule())

        def sbuf_tile(name, width, dtype):
            return sbuf.tile([P, width], dtype, name=name, align_bytes=64)

        def psum_bank(number):
            return psum.tile([P, W], F32, name="bank%d" % number)

        free = {
            "key_wide": [0, 1, 2, 3],
            "key_grouped": [0, 1, 2],
            "val_grouped": [0, 1, 2, 3],
            "sigmoid": [0, 1, 2, 3, 4, 5],
            "att_grouped": [0, 1],
            "y": [0, 1, 2, 3, 4, 5, 6, 7],
            "y_rounded": [0, 1, 2, 3],
            "y_grouped": [0, 1, 2],
            "y_codes": [0, 1, 2, 3],
            "logit_bank": [0, 1, 2],
            "key_bank": [3, 4, 5, 6],
            "y_bank": [7],
            "sum_bank": [],
        }
        key_banks, logit_banks = len(free["key_bank"]), len(free["logit_bank"])
        held, slot_of = {}, {}

        def take(kind, key, width=W, dtype=F32):
            slot = free[kind][0]
            free[kind].remove(slot)
            slot_of[kind, key] = slot
            held[kind, key] = psum_bank(slot) if "bank" in kind else sbuf_tile("%s%d" % (kind, slot), width, dtype)
            return held[kind, key]

        def give(kind, key, to=None):
            free[to or kind].append(slot_of[kind, key])

        def quantize(name, grouped):
            width = grouped.shape[1] // PACK
            codes = sbuf_tile(name + "_codes", width, U32)
            scales = sbuf_tile(name + "_scales", width, U8)
            nc.vector.quantize_mx(out=codes[:].bitcast(FP8X4), scales=scales[:], in_=grouped[:])
            return codes, scales

        def as_planes(ap):
            return ap.rearrange("p (t c i) -> p c t i", i=4, t=PACK)

        def as_grouped(ap):
            return ap.rearrange("p (c i t) -> p c t i", i=4, t=PACK)

        key_bytes, val_planes, gate_tiles, query_codes = {}, {}, {}, {}

        def load_keys(n):
            key_bytes[n] = sbuf_tile("key_bytes%d" % (n % KEY_TILES), 2 * D, U8)
            rows = keys_bytes.rearrange("(G m a t) k -> G a m (t k)", m=P, a=2, t=2)
            nc.sync.dma_start(out=key_bytes[n][:], in_=rows[n // 2, n % 2])

        def load_val_columns(planes, G, first, width):
            nc.sync.dma_start(
                out=planes.rearrange("p (t w) -> p t w", t=PACK),
                in_=vals[G * W : (G + 1) * W, first : first + width].rearrange("(p t) w -> p t w", t=PACK),
            )

        def load_vals(G, h):
            val_planes[G, h] = sbuf_tile("val_planes%d" % G, PACK * W, BF16)
            load_val_columns(val_planes[G, h][:], G, h * W, W)

        def load_gate(b, h):
            gate_tiles[b, h] = sbuf_tile("gate%d" % ((2 * b + h) % GATE_TILES), 4 * W, BF16)
            nc.sync.dma_start(
                out=gate_tiles[b, h][:].rearrange("p (j w) -> p j w", j=4),
                in_=gate[b * W : (b + 1) * W, h * W : (h + 1) * W].rearrange("(j p) w -> p j w", p=P),
            )

        def load_queries(b):
            query_codes[b] = sbuf_tile("query_codes%d" % b, 2 * W, U32)
            words = qry_words.rearrange("g p n t -> p g (n t)")[:, :, b * PACK * W : (b + 1) * PACK * W]
            nc.sync.dma_start(
                out=query_codes[b][:].bitcast(I32).rearrange("p (g n) -> p g n", g=2), in_=words.bitcast(I32)
            )

        def load_per_key(name, row):
            columns = sbuf_tile(name, SLABS, BF16)
            nc.sync.dma_start(
                out=columns[:].rearrange("m (G t) -> m G t", t=PACK),
                in_=row.rearrange("o (G m t) -> m (o G) t", m=P, t=PACK),
            )
            return columns

        scale_columns = sbuf_tile("scale_columns", 8, F32)
        nc.sync.dma_start(
            out=scale_columns[:].rearrange("p (g c) -> p g c", c=4),
            in_=keys_scale.rearrange("o (g p c) -> p (o g) c", p=P, c=4),
        )
        identity = sbuf_tile("identity", P, F32)
        make_identity(nc, identity[:])
        query_scales = sbuf_tile("query_scales", 2 * T, U8)
        nc.gpsimd.memset(query_scales[:].bitcast(I32), 0)
        warm_up = sbuf_tile("warm_up", 1, F32)
        nc.scalar.activation(out=warm_up[:], in_=identity[:, 0:1], func=SIGMOID)

        first_planes = sbuf_tile("val_planes0", PACK * W, BF16)
        piece = [slice(0, 2 * W), slice(2 * W, 4 * W)]
        load_val_columns(first_planes[:, piece[0]], 0, 0, W // 2)
        load_keys(0)
        load_val_columns(first_planes[:, piece[1]], 0, W // 2, W // 2)
        load_vals(1, 0)
        load_keys(1)
        load_keys(2)
        load_vals(2, 0)
        load_keys(3)
        load_vals(3, 0)
        load_queries(0)
        for Q in range(4):
            nc.sync.dma_start(
                out=query_scales[32 * Q : 32 * Q + 4, :].bitcast(I32).rearrange("r (g n) -> r g n", g=2),
                in_=qry_scales[:, 4 * Q : 4 * Q + 4, :].rearrange("g r n -> r g n").bitcast(I32),
            )
        bias = load_per_key("bias", key_bias)
        gain = load_per_key("gain", key_gain)

        scale_rows = sbuf_tile("scale_rows", D, F32)
        for g in range(2):
            spread = psum_bank(g)
            for c in range(4):
                column = scale_columns[:, 4 * g + c : 4 * g + c + 1]
                nc.tensor.transpose(spread[:, c * P : (c + 1) * P], column.to_broadcast([P, P]), identity[:])
            nc.scalar.copy(
                out=scale_rows[:, g * W : (g + 1) * W].rearrange("q (p c) -> q p c", c=4),
                in_=spread[:].rearrange("q (c p) -> q p c", c=4),
            )

        first_grouped = take("val_grouped", (0, 0), PACK * W, BF16)
        nc.vector.tensor_copy(out=as_grouped(first_grouped[:, piece[0]]), in_=as_planes(first_planes[:, piece[0]]))
        nc.scalar.copy(out=as_grouped(first_grouped[:, piece[1]]), in_=as_planes(first_planes[:, piece[1]]))

        key_mx, val_mx, att_mx = {}, {}, {}
        y_scales = sbuf_tile("y_scales", 2 * T, U8)

        def widen_keys(slab):
            wide = take("key_wide", slab, D, BF16)
            values = key_bytes[slab // 2][:, (slab % 2) * D : (slab % 2 + 1) * D].bitcast(FP8)
            for cols in [slice(0, W), slice(W, D)] if slab == 0 else [slice(0, D)]:
                nc.vector.tensor_tensor(out=wide[:, cols], in0=values[:, cols], in1=scale_rows[:, cols], op=MULT)

        def turn_keys(slab):
            words = held["key_wide", slab][:].bitcast(F32)
            bank = take("key_bank", slab)
            for g in range(2):
                for u in range(2):
                    c = 2 * g + u
                    nc.tensor.transpose(
                        bank[:, c * P : (c + 1) * P], words[:, 2 * P * g + u : 2 * P * (g + 1) : 2], identity[:]
                    )
            give("key_wide", slab)

        def group_keys(slab):
            n, second = divmod(slab, 2)
            if not second:
                take("key_grouped", n, 2 * D, BF16)
            words = held["key_grouped", n][:].bitcast(F32)[:, second * W : (second + 1) * W]
            nc.scalar.copy(
                out=words.rearrange("p (g m u) -> p g m u", g=2, u=2),
                in_=held["key_bank", slab][:].rearrange("p (g u m) -> p g m u", g=2, u=2),
            )
            give("key_bank", slab, "sum_bank" if slab >= SLABS - key_banks else None)

        def quantize_keys(n):
            key_mx[n] = quantize("key%d" % n, held["key_grouped", n])
            give("key_grouped", n)

        def group_vals(G, h):
            grouped = take("val_grouped", (G, h), PACK * W, BF16)
            nc.scalar.copy(out=as_grouped(grouped[:]), in_=as_planes(val_planes[G, h][:]))

        def quantize_vals(G, h):
            val_mx[G, h] = quantize("val%d_%d" % (G, h), held["val_grouped", (G, h)])
            give("val_grouped", (G, h))

        def logits(G, b, t):
            codes, scales = key_mx[2 * G + t // 2]
            bank = take("logit_bank", (G, b, t))
            for g in range(2):
                keys = slice((2 * (t % 2) + g) * P, (2 * (t % 2) + g + 1) * P)
                nc.tensor.matmul_mx(
                    out=bank[:],
                    lhsT=codes[:, keys].bitcast(FP8X4),
                    lhsT_scale=scales[:, keys],
                    rhs=query_codes[b][:, g * W : (g + 1) * W].bitcast(FP8X4),
                    rhs_scale=query_scales[:, g * T + b * W : g * T + (b + 1) * W],
                    start=(g == 0),
                    stop=(g == 1),
                )

        def sigmoid(G, b, t):
            if t == 0:
                take("sigmoid", (G, b), PACK * W, F32)
            nc.scalar.activation(
                out=held["sigmoid", (G, b)][:, t * W : (t + 1) * W],
                in_=held["logit_bank", (G, b, t)][:],
                func=SIGMOID,
                bias=bias[:, PACK * G + t : PACK * G + t + 1],
            )
            retired = t - (PACK - logit_banks) if (G, b) == (GROUPS - 1, 1) else -1
            give("logit_bank", (G, b, t), None if retired < 0 else "y_bank" if retired == 0 else "sum_bank")

        def apply_gain(G, b):
            grouped = take("att_grouped", (G, b), PACK * W, BF16)
            gains = gain[:, PACK * G : PACK * (G + 1)].unsqueeze(1).unsqueeze(3)
            nc.vector.tensor_tensor(
                out=as_grouped(grouped[:]),
                in0=as_planes(held["sigmoid", (G, b)][:]),
                in1=gains.to_broadcast([P, W // 4, PACK, 4]),
                op=MULT,
            )
            give("sigmoid", (G, b))

        def quantize_att(G, b):
            att_mx[G, b] = quantize("att%d_%d" % (G, b), held["att_grouped", (G, b)])
            give("att_grouped", (G, b))

        def mix(j, h, G):
            if G == 0:
                take("sum_bank", (j, h))
            att_codes, att_scales = att_mx[G, j // 4]
            val_codes, val_scales = val_mx[G, h]
            queries = slice((j % 4) * P, (j % 4 + 1) * P)
            nc.tensor.matmul_mx(
                out=held["sum_bank", (j, h)][:],
                lhsT=att_codes[:, queries].bitcast(FP8X4),
                lhsT_scale=att_scales[:, queries],
                rhs=val_codes[:].bitcast(FP8X4),
                rhs_scale=val_scales[:],
                start=(G == 0),
                stop=(G == GROUPS - 1),
            )

        def apply_gate(j, h):
            y = take("y", (j, h))
            nc.vector.tensor_tensor(
                out=y[:],
                in0=held["sum_bank", (j, h)][:],
                in1=gate_tiles[j // 4, h][:, (j % 4) * W : (j % 4 + 1) * W],
                op=MULT,
            )
            give("sum_bank", (j, h))
            nc.sync.dma_start(out=out_0[j * P : (j + 1) * P, h * W : (h + 1) * W], in_=y[:])

        def round_y(j, h):
            rounded = take("y_rounded", (j, h), W, BF16)
            cast = nc.vector.tensor_copy if (j, h) in last_pair else nc.scalar.copy
            cast(
                out=rounded[:].rearrange("p (u m e) -> p u m e", u=2, e=2),
                in_=held["y", (j, h)][:].rearrange("p (m u e) -> p u m e", u=2, e=2),
            )
            give("y", (j, h))

        def turn_y(j, h):
            if j % 2 == 0:
                take("y_bank", (j // 2, h))
            words = held["y_rounded", (j, h)][:].bitcast(F32)
            for u in range(2):
                c = 2 * (j % 2) + u
                nc.tensor.transpose(
                    held["y_bank", (j // 2, h)][:, c * P : (c + 1) * P], words[:, u * P : (u + 1) * P], identity[:]
                )
            give("y_rounded", (j, h))

        def group_y(r, h):
            grouped = take("y_grouped", (r, h), 2 * W, BF16)
            nc.scalar.copy(
                out=grouped[:].bitcast(F32).rearrange("p (j m u) -> p j m u", j=2, u=2),
                in_=held["y_bank", (r, h)][:].rearrange("p (j u m) -> p j m u", j=2, u=2),
            )
            give("y_bank", (r, h))

        def quantize_y(r, h):
            codes = take("y_codes", (r, h), 2 * P, U32)
            nc.vector.quantize_mx(
                out=codes[:].bitcast(FP8X4),
                scales=y_scales[:, h * T + r * 2 * P : h * T + (r + 1) * 2 * P],
                in_=held["y_grouped", (r, h)][:],
            )
            give("y_grouped", (r, h))
            words = out_1[h].rearrange("p m t -> p (m t)")[:, r * 2 * P * PACK : (r + 1) * 2 * P * PACK]
            nc.sync.dma_start(out=words.bitcast(I32), in_=codes[:].bitcast(I32))
            give("y_codes", (r, h))

        before = {
            load_keys: lambda n: ([(widen_keys, 2 * (n - KEY_TILES) + 1)], None),
            load_vals: lambda G, h: ([(group_vals, G, 0)], None),
            load_queries: lambda b: ([], None),
            load_gate: lambda b, h: ([(apply_gate, 3, 0)] if (b, h) == (1, 1) else [], None),
            widen_keys: lambda slab: ([(load_keys, slab // 2)], "key_wide"),
            turn_keys: lambda slab: ([(widen_keys, slab)], "key_bank"),
            group_keys: lambda slab: ([(turn_keys, slab)], None if slab % 2 else "key_grouped"),
            quantize_keys: lambda n: ([(group_keys, 2 * n + 1)], None),
            group_vals: lambda G, h: ([(load_vals, G, h)], "val_grouped"),
            quantize_vals: lambda G, h: ([(group_vals, G, h)], None),
            logits: lambda G, b, t: ([(quantize_keys, 2 * G + t // 2), (load_queries, b)], "logit_bank"),
            sigmoid: lambda G, b, t: ([(logits, G, b, t)], None if t else "sigmoid"),
            apply_gain: lambda G, b: ([(sigmoid, G, b, PACK - 1)], "att_grouped"),
            quantize_att: lambda G, b: ([(apply_gain, G, b)], None),
            mix: lambda j, h, G: ([(quantize_att, G, j // 4), (quantize_vals, G, h)], None if G else "sum_bank"),
            apply_gate: lambda j, h: ([(mix, j, h, GROUPS - 1), (load_gate, j // 4, h)], "y"),
            round_y: lambda j, h: ([(apply_gate, j, h)], "y_rounded"),
            turn_y: lambda j, h: ([(round_y, j, h)], None if j % 2 else "y_bank"),
            group_y: lambda r, h: ([(turn_y, 2 * r + 1, h)], "y_grouped"),
            quantize_y: lambda r, h: ([(group_y, r, h)], "y_codes"),
        }
        done = {(load_keys, n) for n in range(KEY_TILES)} | {(load_vals, G, 0) for G in range(GROUPS)}
        done = done | {(load_queries, 0), (group_vals, 0, 0)}

        def each(step, arguments):
            return [(step, *a) for a in arguments]

        def slabs_of(G, b):
            return [(G, b, t) for t in range(PACK)]

        def passes(units, groups):
            return [(mix, j, h, G) for G in groups for j, h in units]

        set_a, set_b, set_c, set_d = [[(4 * b + j, h) for j in range(4)] for b in range(2) for h in range(2)]
        last_pair = set_d[2:]

        loads = [(load_keys, 4), (load_keys, 5), (load_queries, 1), (load_keys, 6), (load_keys, 7)]
        loads += [(load_vals, G, 1) for G in range(GROUPS)]
        loads += each(load_gate, [(0, 0), (0, 1), (1, 0), (1, 1)])

        vector = []
        for n in range(PAIRS):
            vector += [(widen_keys, 2 * n), (widen_keys, 2 * n + 1)]
            if n >= QUANTIZE_LAG:
                vector += [(quantize_keys, n - QUANTIZE_LAG)]
        vector += [(apply_gain, 0, 0), (quantize_keys, PAIRS - 2), (quantize_vals, 0, 0), (quantize_keys, PAIRS - 1)]
        vector += [(quantize_att, 0, 0)]
        for G in range(1, GROUPS):
            vector += [(apply_gain, G, 0), (quantize_vals, G, 0), (quantize_att, G, 0)]
        vector += [(quantize_vals, 0, 1)] + each(apply_gate, set_a) + [(quantize_vals, 1, 1), (quantize_vals, 2, 1)]
        vector += [(apply_gain, 0, 1), (quantize_vals, 3, 1), (quantize_att, 0, 1)]
        vector += [(apply_gain, 1, 1)] + each(apply_gate, set_b[:2]) + [(quantize_att, 1, 1)]
        vector += each(apply_gate, set_b[2:])
        vector += [(apply_gain, 2, 1), (quantize_y, 0, 0), (quantize_att, 2, 1)]
        vector += [(apply_gain, 3, 1), (quantize_y, 1, 0), (quantize_att, 3, 1), (quantize_y, 0, 1), (quantize_y, 1, 1)]
        vector += each(apply_gate, set_c + set_d) + each(round_y, last_pair)
        vector += each(quantize_y, [(2, 0), (3, 0), (2, 1), (3, 1)])

        between = [[(group_vals, 2, 0)], [(group_vals, 3, 0)]]
        for G in range(GROUPS - 1):
            between += [[], each(sigmoid, slabs_of(G, 0))]
        scalar = [(group_vals, 1, 0)]
        for n in range(PAIRS):
            scalar += [(group_keys, 2 * n), (group_keys, 2 * n + 1)] + between[n]
        early_logits = slabs_of(0, 1) + slabs_of(3, 0) + slabs_of(1, 1)
        scalar += each(sigmoid, early_logits) + [(group_vals, G, 1) for G in range(GROUPS)]
        scalar += each(sigmoid, slabs_of(2, 1)) + each(round_y, set_a[:2])
        scalar += each(sigmoid, slabs_of(3, 1)) + each(round_y, set_a[2:])
        scalar += [(group_y, 0, 0)] + each(round_y, set_b[:2]) + [(group_y, 1, 0)] + each(round_y, set_b[2:])
        scalar += [(group_y, 0, 1), (group_y, 1, 1)]
        scalar += each(round_y, set_c) + [(group_y, 2, 0)] + each(round_y, set_d[:2])
        scalar += each(group_y, [(3, 0), (2, 1), (3, 1)])

        tensor = []
        for n in range(PAIRS):
            tensor += [(turn_keys, 2 * n), (turn_keys, 2 * n + 1)]
            tensor += [(logits, *step[1:]) for step in between[n] if step[0] is sigmoid]
        late_logits = each(logits, slabs_of(2, 1) + slabs_of(3, 1))
        tensor += each(logits, early_logits) + late_logits[:logit_banks] + passes(set_a, range(GROUPS))
        tensor += passes(set_b, range(3)) + late_logits[logit_banks : 2 * logit_banks]
        tensor += passes(set_b, [3]) + late_logits[2 * logit_banks :] + each(turn_y, set_a[:2])
        open_units = set_c + set_d[:2]
        tensor += passes(open_units[:2], [0]) + each(turn_y, set_a[2:]) + passes(open_units[2:], [0])
        tensor += passes(open_units, [1]) + each(turn_y, set_b) + passes(open_units, [2, 3])
        tensor += passes(last_pair[:1], range(GROUPS)) + each(turn_y, set_c[:2])
        tensor += passes(last_pair[1:], range(GROUPS)) + each(turn_y, set_c[2:] + set_d)

        queues = [loads, scalar, vector, tensor]
        while any(queues):
            written = len(done)
            for queue in queues:
                while queue:
                    step = queue[0]
                    earlier, kind = before[step[0]](*step[1:])
                    if not all(other in done for other in earlier) or (kind and not free[kind]):
                        break
                    queue.remove(step)
                    step[0](*step[1:])
                    done.add(step)
            assert len(done) > written

        for Q in range(4):
            engine = nc.sync if Q % 2 == 0 else nc.scalar
            engine.dma_start(
                out=out_2[:, 4 * Q : 4 * Q + 4, :].rearrange("h r m -> r h m").bitcast(I32),
                in_=y_scales[32 * Q : 32 * Q + 4, :].bitcast(I32).rearrange("r (h m) -> r h m", h=2),
            )
